import numpy as np
import ml_dtypes


def mxq(x, axis, fmt="e4m3"):
    dtype, down = {"e4m3": (ml_dtypes.float8_e4m3fn, 7), "e5m2": (ml_dtypes.float8_e5m2, 14)}[fmt]
    v = np.moveaxis(np.asarray(x, np.float32).astype(ml_dtypes.bfloat16).astype(np.float64), axis, -1)
    blocks = v.reshape(v.shape[:-1] + (-1, 32))
    amax = np.abs(blocks).max(-1, keepdims=True)
    byte = np.maximum(np.where(amax > 0, np.frexp(amax)[1] - 1 + 127, 0) - down, 1)
    scale = np.exp2(byte - 127.0)
    codes = (blocks / scale).astype(np.float32).astype(dtype).astype(np.float64)
    return np.moveaxis((codes * scale).reshape(v.shape), -1, axis)


WIDE = False


def mx_kscale(k):
    if not WIDE:
        return np.ones(k)
    levels = np.array([10, -10, 5, -5, 0])
    if k % 512:
        return np.exp2(np.random.permutation(np.resize(levels, k // 32))).repeat(32)
    a = np.empty((k // 512, 16))
    for p in range(k // 512):
        a[p, :8] = np.random.permutation(np.resize(levels, 8))
        for g in range(8):
            far = levels[np.abs(levels - a[p, g]) >= 10]
            a[p, g + 8] = far[np.random.randint(len(far))]
    return np.exp2(a.ravel()).repeat(32)


def f64(x):
    return np.asarray(x).astype(np.float64)


def striped(idx):
    return np.tile(idx.reshape(-1, 16).T, (8, 1)).astype(np.uint16)


def unstriped(offs):
    return offs[:16].T.reshape(-1).astype(np.int64)


def relu(v):
    return np.maximum(v, 0.0)


K, T, E, C, N = 1536, 512, 8, 128, 128


def by_expert(wq, xq):
    return np.concatenate([wq[e].T @ xq[:, e * C:(e + 1) * C] for e in range(E)], axis=1)


def setup_inputs():
    n = np.random.standard_normal
    s = mx_kscale(K)[:, None]
    first = np.random.permutation(np.repeat(np.arange(E), T // E))
    second = (first + 1 + np.random.permutation(np.repeat(np.arange(E - 1), -(-T // (E - 1)))[:T])) % E
    while np.bincount(second, minlength=E).max() != T // E:
        load = np.bincount(second, minlength=E); hi, lo = int(load.argmax()), int(load.argmin())
        t = np.flatnonzero((second == hi) & (first != lo))[0]; second[t] = lo
    slot_token = np.empty(E * C, np.int64); pos = np.empty((2, T), np.int64); fill = np.zeros(E, np.int64)
    place = np.stack([np.random.permutation(C) for _ in range(E)])
    for r, deal in enumerate((first, second)):
        for t in np.random.permutation(T):
            e = deal[t]; j = e * C + place[e, fill[e]]; fill[e] += 1; slot_token[j] = t; pos[r, t] = j
    g = np.random.uniform(0.2, 0.8, T)
    return {
        "xT": (n((K, T)) * s).astype(np.float32),
        "w": (n((E, K, N)) / np.sqrt(K) / s[None]).astype(np.float32),
        "b": (0.3 * n((N, E))).astype(np.float32),
        "gate": np.stack([np.tile(g, (N, 1)), np.tile(1.0 - g, (N, 1))]).astype(np.float32),
        "offs": striped(slot_token),
        "pos1": striped(pos[0]),
        "pos2": striped(pos[1]),
    }


def reference(xT, w, b, gate, offs, pos1, pos2):
    idx = unstriped(offs)
    xq = mxq(f64(xT)[:, idx], 0, "e4m3")
    y = by_expert(mxq(f64(w), 1, "e4m3"), xq)
    y = relu(y + np.repeat(f64(b), C, axis=1))
    return f64(gate[0]) * y[:, unstriped(pos1)] + f64(gate[1]) * y[:, unstriped(pos2)]

@@ -1,0 +1,162 @@
+from contextlib import ExitStack
+
+import concourse.mybir as mybir
+
+K, T, E, C, N = 1536, 512, 8, 128, 128
+P = 128
+PACK = 4
+A = K // (P * PACK)
+SLOTS = E * C
+
+FLOPS = 2 * K * N * SLOTS
+
+F32 = mybir.dt.float32
+BF16 = mybir.dt.bfloat16
+I32 = mybir.dt.int32
+U32 = mybir.dt.uint32
+U16 = mybir.dt.uint16
+U8 = mybir.dt.uint8
+FP8X4 = mybir.dt.float8_e4m3fn_x4
+RELU = mybir.ActivationFunctionType.Relu
+ADD = mybir.AluOpType.add
+MAX = mybir.AluOpType.max
+MULT = mybir.AluOpType.mult
+
+WINDOW = 1408
+
+SCALE_ROW = 4
+
+X_SHARES = (
+    (("vector", 0, 320), ("scalar", 320, 512)),
+    (("scalar", 0, 384), ("vector", 384, 512)),
+    (("scalar", 0, 512),),
+)
+
+W_GROUPS = ((4, 0), (4, 0), (4, 0), (3, 1), (2, 0), (0, 2), (0, 2), (0, 1), (0, 1))
+
+REUSED_GROUP = 4
+
+POS_AFTER_GROUP = 2
+
+OUT_CUTS = ((0, 320), (320, 512))
+
+
+def tile_routed_moe_kernel(tc, xT, w, b, gate, offs, pos1, pos2, out):
+    nc = tc.nc
+    engine_copy = {"vector": nc.vector.tensor_copy, "scalar": nc.scalar.copy}
+
+    with ExitStack() as ctx:
+        keep = ctx.enter_context(tc.tile_pool(name="keep", bufs=1))
+        psum = ctx.enter_context(tc.psum_pool(name="psum", bufs=1))
+
+        offs_tile = keep.tile([P, SLOTS // 16], U16, name="offs_tile")
+        pos1_tile = keep.tile([P, T // 16], U16, name="pos1_tile")
+        pos2_tile = keep.tile([P, T // 16], U16, name="pos2_tile")
+        bias = keep.tile([P, E], F32, name="bias")
+        gates = keep.tile([P, 2, T], F32, name="gates")
+
+        x_rows = xT.rearrange("(a p t) n -> a p t n", p=P, t=PACK)
+        x_raw = []
+        for a in range(A):
+            raw = keep.tile([P, PACK, T], F32, name=f"x_raw_{a}")
+            nc.sync.dma_start(out=raw[:], in_=x_rows[a])
+            x_raw.append(raw)
+            if a == 0:
+                nc.sync.dma_start(offs_tile[:], offs)
+        nc.sync.dma_start(out=bias[:], in_=b)
+        w_rows = w.flatten_outer_dims().rearrange("(u p t) n -> p u (t n)", p=P, t=PACK)
+        w_raw = []
+        first = 0
+        for i, shares in enumerate(W_GROUPS):
+            blocks = sum(shares)
+            tag = "reused" if i == REUSED_GROUP else f"w_raw_{i}"
+            raw = keep.tile([P, blocks, PACK * N], F32, name=f"w_raw_{i}", tag=tag)
+            nc.sync.dma_start(out=raw[:], in_=w_rows[:, first : first + blocks, :])
+            w_raw.append(raw)
+            first += blocks
+            if i == POS_AFTER_GROUP:
+                nc.sync.dma_start(pos1_tile[:], pos1)
+                nc.sync.dma_start(pos2_tile[:], pos2)
+        nc.sync.dma_start(out=gates[:], in_=gate.rearrange("r n t -> n r t"))
+
+        x_scales = keep.tile([P, WINDOW], U8, name="x_scales", align_bytes=64)
+        nc.gpsimd.memset(x_scales[:], 0)
+        x_words = []
+        for a in range(A):
+            words = keep.tile([P, WINDOW], U32, name=f"x_words_{a}", align_bytes=64)
+            nc.vector.memset(words[:, T:WINDOW].bitcast(I32), 0)
+            x_words.append(words)
+
+        slot_words = keep.tile([P, A, SLOTS], U32, name="slot_words", align_bytes=64)
+        slot_scales = keep.tile([P, SLOTS], U8, name="slot_scales", align_bytes=64)
+        for a in range(A):
+            grouped = keep.tile([P, T, PACK], BF16, name=f"x_grouped_{a}", align_bytes=64)
+            for engine, lo, hi in X_SHARES[a]:
+                engine_copy[engine](
+                    out=grouped[:, lo:hi, :].rearrange("p (c i) t -> p c t i", i=4),
+                    in_=x_raw[a][:, :, lo:hi].rearrange("p t (c i) -> p c t i", i=4),
+                )
+            nc.vector.quantize_mx(
+                out=x_words[a][:, 0:T].bitcast(FP8X4),
+                scales=x_scales[SCALE_ROW * a : P, 0:T],
+                in_=grouped[:].rearrange("p n t -> p (n t)"),
+            )
+            nc.vector.tensor_copy(slot_words[:, a, :], x_words[a][:].indirect(offs_tile[:]))
+        nc.vector.tensor_copy(slot_scales[:], x_scales[:].indirect(offs_tile[:]))
+
+        sums = []
+        block = 0
+        for i, (scalar_blocks, vector_blocks) in enumerate(W_GROUPS):
+            blocks = scalar_blocks + vector_blocks
+            grouped = keep.tile([P, blocks, N, PACK], BF16, name=f"w_grouped_{i}", align_bytes=64)
+            for engine, lo, hi in (("scalar", 0, scalar_blocks), ("vector", scalar_blocks, blocks)):
+                if lo < hi:
+                    engine_copy[engine](
+                        out=grouped[:, lo:hi].rearrange("p u (c i) t -> p u c t i", i=4),
+                        in_=w_raw[i][:, lo:hi].rearrange("p u (t c i) -> p u c t i", t=PACK, i=4),
+                    )
+            w_words = keep.tile([P, blocks * N], U32, name=f"w_words_{i}", align_bytes=64)
+            w_scales = keep.tile([P, blocks * N], U8, name=f"w_scales_{i}", align_bytes=64)
+            nc.vector.quantize_mx(
+                out=w_words[:].bitcast(FP8X4),
+                scales=w_scales[:],
+                in_=grouped[:].rearrange("p u n t -> p (u n t)"),
+            )
+            for j in range(blocks):
+                e, a = divmod(block, A)
+                if a == 0:
+                    sums.append(psum.tile([N, C], F32, name=f"sums_{e}"))
+                features = slice(j * N, (j + 1) * N)
+                places = slice(e * C, (e + 1) * C)
+                nc.tensor.matmul_mx(
+                    out=sums[e][:],
+                    lhsT=w_words[:, features].bitcast(FP8X4),
+                    lhsT_scale=w_scales[:, features],
+                    rhs=slot_words[:, a, places].bitcast(FP8X4),
+                    rhs_scale=slot_scales[SCALE_ROW * a : P, places],
+                    start=(a == 0),
+                    stop=(a == A - 1),
+                )
+                block += 1
+
+        results = keep.tile([P, SLOTS], F32, name="results", tag="reused")
+        for e in range(E):
+            places = slice(e * C, (e + 1) * C)
+            if e < E - 1:
+                nc.scalar.activation(results[:, places], sums[e][:], RELU, bias=bias[:, e : e + 1])
+            else:
+                nc.vector.tensor_scalar(results[:, places], sums[e][:], bias[:, e : e + 1], 0.0, ADD, MAX)
+
+        y1 = keep.tile([P, T], F32, name="y1")
+        nc.vector.tensor_tensor(y1[:], results[:].indirect(pos1_tile[:]), gates[:, 0, :], MULT)
+        y2 = []
+        for lo, hi in OUT_CUTS:
+            part = keep.tile([P, hi - lo], F32, name=f"y2_{lo}")
+            nc.vector.tensor_tensor(
+                part[:], results[:].indirect(pos2_tile[:, lo // 16 : hi // 16]), gates[:, 1, lo:hi], MULT
+            )
+            y2.append(part)
+        for (lo, hi), part in zip(OUT_CUTS, y2):
+            y = keep.tile([P, hi - lo], F32, name=f"y_{lo}")
+            nc.vector.tensor_tensor(y[:], y1[:, lo:hi], part[:], ADD)
+            nc.sync.dma_start(out=out[:, lo:hi], in_=y[:])

@@ -26,24 +26,30 @@ WINDOW = 1408
 
 SCALE_ROW = 4
 
-X_SHARES = (
-    (("vector", 0, 320), ("scalar", 320, 512)),
-    (("scalar", 0, 384), ("vector", 384, 512)),
-    (("scalar", 0, 512),),
-)
+X_LOADS = (((0, 256, 160), (256, 512, 160)), ((0, 256, 0), (256, 512, 0)), ((0, 256, 0), (256, 512, 0)))
 
-W_GROUPS = ((4, 0), (4, 0), (4, 0), (3, 1), (2, 0), (0, 2), (0, 2), (0, 1), (0, 1))
+X_QUANT = (((0, 256), (256, 512)), ((0, 512),), ((0, 512),))
 
-REUSED_GROUP = 4
+W_GROUPS = ((0, 2, 0), (2, 2, 0), (4, 2, 0), (6, 2, 0), (8, 2, 0), (10, 2, 0), (12, 2, 0), (14, 2, 0), (16, 2, 256), (18, 2, 0), (21, 2, 128), (20, 1, 0), (23, 1, 64))
 
-POS_AFTER_GROUP = 2
+W_QUANT = (4, 4, 4, 2, 2, 2, 2, 2, 1, 1)
+
+REUSED_GROUP = 7
+
+VECTOR_RELUS = (4, 5, 6)
 
 OUT_CUTS = ((0, 320), (320, 512))
 
 
 def tile_routed_moe_kernel(tc, xT, w, b, gate, offs, pos1, pos2, out):
     nc = tc.nc
-    engine_copy = {"vector": nc.vector.tensor_copy, "scalar": nc.scalar.copy}
+
+    def interleave(grouped, raw, lo, hi, copy):
+        if lo < hi:
+            copy(
+                out=grouped[:, lo:hi, :].rearrange("p (c i) t -> p c t i", i=4),
+                in_=raw[:, :, lo:hi].rearrange("p t (c i) -> p c t i", i=4),
+            )
 
     with ExitStack() as ctx:
         keep = ctx.enter_context(tc.tile_pool(name="keep", bufs=1))
@@ -53,68 +59,78 @@ def tile_routed_moe_kernel(tc, xT, w, b, gate, offs, pos1, pos2, out):
         pos1_tile = keep.tile([P, T // 16], U16, name="pos1_tile")
         pos2_tile = keep.tile([P, T // 16], U16, name="pos2_tile")
         bias = keep.tile([P, E], F32, name="bias")
-        gates = keep.tile([P, 2, T], F32, name="gates")
+        gate1 = keep.tile([P, T], F32, name="gate1")
+        gate2 = keep.tile([P, T], F32, name="gate2")
 
         x_rows = xT.rearrange("(a p t) n -> a p t n", p=P, t=PACK)
         x_raw = []
         for a in range(A):
-            raw = keep.tile([P, PACK, T], F32, name=f"x_raw_{a}")
-            nc.sync.dma_start(out=raw[:], in_=x_rows[a])
-            x_raw.append(raw)
+            for lo, hi, vector_tokens in X_LOADS[a]:
+                raw = keep.tile([P, PACK, hi - lo], F32, name=f"x_raw_{a}_{lo}")
+                nc.sync.dma_start(out=raw[:], in_=x_rows[a][:, :, lo:hi])
+                x_raw.append(raw)
             if a == 0:
                 nc.sync.dma_start(offs_tile[:], offs)
         nc.sync.dma_start(out=bias[:], in_=b)
         w_rows = w.flatten_outer_dims().rearrange("(u p t) n -> p u (t n)", p=P, t=PACK)
         w_raw = []
-        first = 0
-        for i, shares in enumerate(W_GROUPS):
-            blocks = sum(shares)
+        for i, (first, blocks, vector_columns) in enumerate(W_GROUPS):
             tag = "reused" if i == REUSED_GROUP else f"w_raw_{i}"
-            raw = keep.tile([P, blocks, PACK * N], F32, name=f"w_raw_{i}", tag=tag)
-            nc.sync.dma_start(out=raw[:], in_=w_rows[:, first : first + blocks, :])
+            raw = keep.tile([P, blocks, PACK, N], F32, name=f"w_raw_{i}", tag=tag)
+            nc.sync.dma_start(out=raw[:].rearrange("p u t n -> p u (t n)"), in_=w_rows[:, first : first + blocks, :])
             w_raw.append(raw)
-            first += blocks
-            if i == POS_AFTER_GROUP:
-                nc.sync.dma_start(pos1_tile[:], pos1)
-                nc.sync.dma_start(pos2_tile[:], pos2)
-        nc.sync.dma_start(out=gates[:], in_=gate.rearrange("r n t -> n r t"))
+        nc.sync.dma_start(pos1_tile[:], pos1)
+        nc.sync.dma_start(out=gate1[:], in_=gate[0])
+        nc.sync.dma_start(pos2_tile[:], pos2)
+        nc.sync.dma_start(out=gate2[:], in_=gate[1])
 
         x_scales = keep.tile([P, WINDOW], U8, name="x_scales", align_bytes=64)
-        nc.gpsimd.memset(x_scales[:], 0)
-        x_words = []
-        for a in range(A):
-            words = keep.tile([P, WINDOW], U32, name=f"x_words_{a}", align_bytes=64)
-            nc.vector.memset(words[:, T:WINDOW].bitcast(I32), 0)
-            x_words.append(words)
+        nc.vector.memset(x_scales[:].bitcast(I32), 0)
+        x_words = keep.tile([P, (A - 1) * T + WINDOW], U32, name="x_words", align_bytes=64)
+        nc.vector.memset(x_words[:, A * T :].bitcast(I32), 0)
 
         slot_words = keep.tile([P, A, SLOTS], U32, name="slot_words", align_bytes=64)
         slot_scales = keep.tile([P, SLOTS], U8, name="slot_scales", align_bytes=64)
+        piece = 0
         for a in range(A):
             grouped = keep.tile([P, T, PACK], BF16, name=f"x_grouped_{a}", align_bytes=64)
-            for engine, lo, hi in X_SHARES[a]:
-                engine_copy[engine](
-                    out=grouped[:, lo:hi, :].rearrange("p (c i) t -> p c t i", i=4),
-                    in_=x_raw[a][:, :, lo:hi].rearrange("p t (c i) -> p c t i", i=4),
+            for lo, hi, vector_tokens in X_LOADS[a]:
+                interleave(grouped[:, lo:hi, :], x_raw[piece], 0, vector_tokens, nc.vector.tensor_copy)
+                interleave(grouped[:, lo:hi, :], x_raw[piece], vector_tokens, hi - lo, nc.scalar.copy)
+                piece += 1
+            start = (A - 1 - a) * T
+            for lo, hi in X_QUANT[a]:
+                nc.vector.quantize_mx(
+                    out=x_words[:, start + lo : start + hi].bitcast(FP8X4),
+                    scales=x_scales[SCALE_ROW * a : P, lo:hi],
+                    in_=grouped[:, lo:hi, :].rearrange("p n t -> p (n t)"),
                 )
-            nc.vector.quantize_mx(
-                out=x_words[a][:, 0:T].bitcast(FP8X4),
-                scales=x_scales[SCALE_ROW * a : P, 0:T],
-                in_=grouped[:].rearrange("p n t -> p (n t)"),
-            )
-            nc.vector.tensor_copy(slot_words[:, a, :], x_words[a][:].indirect(offs_tile[:]))
+            nc.vector.tensor_copy(slot_words[:, a, :], x_words[:, start : start + WINDOW].indirect(offs_tile[:]))
         nc.vector.tensor_copy(slot_scales[:], x_scales[:].indirect(offs_tile[:]))
 
-        sums = []
-        block = 0
-        for i, (scalar_blocks, vector_blocks) in enumerate(W_GROUPS):
-            blocks = scalar_blocks + vector_blocks
+        sums = [psum.tile([N, C], F32, name=f"sums_{e}") for e in range(E)]
+        load = 0
+        for i, blocks in enumerate(W_QUANT):
             grouped = keep.tile([P, blocks, N, PACK], BF16, name=f"w_grouped_{i}", align_bytes=64)
-            for engine, lo, hi in (("scalar", 0, scalar_blocks), ("vector", scalar_blocks, blocks)):
-                if lo < hi:
-                    engine_copy[engine](
-                        out=grouped[:, lo:hi].rearrange("p u (c i) t -> p u c t i", i=4),
-                        in_=w_raw[i][:, lo:hi].rearrange("p u (t c i) -> p u c t i", t=PACK, i=4),
-                    )
+            filled = 0
+            members = []
+            while filled < blocks:
+                first, loaded, vector_columns = W_GROUPS[load]
+                target = grouped[:, filled : filled + loaded]
+                if loaded == 1:
+                    interleave(target[:, 0], w_raw[load][:, 0], 0, N - vector_columns, nc.scalar.copy)
+                    interleave(target[:, 0], w_raw[load][:, 0], N - vector_columns, N, nc.vector.tensor_copy)
+                else:
+                    split = loaded - vector_columns // N
+                    for copy, lo, hi in ((nc.scalar.copy, 0, split), (nc.vector.tensor_copy, split, loaded)):
+                        if lo < hi:
+                            copy(
+                                out=target[:, lo:hi].rearrange("p u (c i) t -> p u c t i", i=4),
+                                in_=w_raw[load][:, lo:hi].rearrange("p u t (c i) -> p u c t i", i=4),
+                            )
+                members.extend(range(first, first + loaded))
+                filled += loaded
+                load += 1
             w_words = keep.tile([P, blocks * N], U32, name=f"w_words_{i}", align_bytes=64)
             w_scales = keep.tile([P, blocks * N], U8, name=f"w_scales_{i}", align_bytes=64)
             nc.vector.quantize_mx(
@@ -122,10 +138,8 @@ def tile_routed_moe_kernel(tc, xT, w, b, gate, offs, pos1, pos2, out):
                 scales=w_scales[:],
                 in_=grouped[:].rearrange("p u n t -> p (u n t)"),
             )
-            for j in range(blocks):
+            for j, block in enumerate(members):
                 e, a = divmod(block, A)
-                if a == 0:
-                    sums.append(psum.tile([N, C], F32, name=f"sums_{e}"))
                 features = slice(j * N, (j + 1) * N)
                 places = slice(e * C, (e + 1) * C)
                 nc.tensor.matmul_mx(
@@ -137,24 +151,21 @@ def tile_routed_moe_kernel(tc, xT, w, b, gate, offs, pos1, pos2, out):
                     start=(a == 0),
                     stop=(a == A - 1),
                 )
-                block += 1
 
         results = keep.tile([P, SLOTS], F32, name="results", tag="reused")
         for e in range(E):
             places = slice(e * C, (e + 1) * C)
-            if e < E - 1:
-                nc.scalar.activation(results[:, places], sums[e][:], RELU, bias=bias[:, e : e + 1])
-            else:
+            if e in VECTOR_RELUS:
                 nc.vector.tensor_scalar(results[:, places], sums[e][:], bias[:, e : e + 1], 0.0, ADD, MAX)
+            else:
+                nc.scalar.activation(results[:, places], sums[e][:], RELU, bias=bias[:, e : e + 1])
 
         y1 = keep.tile([P, T], F32, name="y1")
-        nc.vector.tensor_tensor(y1[:], results[:].indirect(pos1_tile[:]), gates[:, 0, :], MULT)
+        nc.vector.tensor_tensor(y1[:], results[:].indirect(pos1_tile[:]), gate1[:], MULT)
         y2 = []
         for lo, hi in OUT_CUTS:
             part = keep.tile([P, hi - lo], F32, name=f"y2_{lo}")
-            nc.vector.tensor_tensor(
-                part[:], results[:].indirect(pos2_tile[:, lo // 16 : hi // 16]), gates[:, 1, lo:hi], MULT
-            )
+            nc.vector.tensor_tensor(part[:], results[:].indirect(pos2_tile[:, lo // 16 : hi // 16]), gate2[:, lo:hi], MULT)
             y2.append(part)
         for (lo, hi), part in zip(OUT_CUTS, y2):
             y = keep.tile([P, hi - lo], F32, name=f"y_{lo}")

@@ -26,9 +26,9 @@ WINDOW = 1408
 
 SCALE_ROW = 4
 
-X_LOADS = (((0, 256, 160), (256, 512, 160)), ((0, 256, 0), (256, 512, 0)), ((0, 256, 0), (256, 512, 0)))
+X_LOADS = (((0, 512, 320),), ((0, 512, 128),), ((0, 512, 0),))
 
-X_QUANT = (((0, 256), (256, 512)), ((0, 512),), ((0, 512),))
+X_QUANT = (((0, 512),), ((0, 512),), ((0, 512),))
 
 W_GROUPS = ((0, 2, 0), (2, 2, 0), (4, 2, 0), (6, 2, 0), (8, 2, 0), (10, 2, 0), (12, 2, 0), (14, 2, 0), (16, 2, 256), (18, 2, 0), (21, 2, 128), (20, 1, 0), (23, 1, 64))
 

@@ -26,33 +26,15 @@ WINDOW = 1408
 
 SCALE_ROW = 4
 
-X_LOADS = (((0, 512, 320),), ((0, 512, 128),), ((0, 512, 0),))
-
-X_QUANT = (((0, 512),), ((0, 512),), ((0, 512),))
-
-W_GROUPS = ((0, 2, 0), (2, 2, 0), (4, 2, 0), (6, 2, 0), (8, 2, 0), (10, 2, 0), (12, 2, 0), (14, 2, 0), (16, 2, 256), (18, 2, 0), (21, 2, 128), (20, 1, 0), (23, 1, 64))
-
-W_QUANT = (4, 4, 4, 2, 2, 2, 2, 2, 1, 1)
-
-REUSED_GROUP = 7
-
-VECTOR_RELUS = (4, 5, 6)
-
 OUT_CUTS = ((0, 320), (320, 512))
 
 
 def tile_routed_moe_kernel(tc, xT, w, b, gate, offs, pos1, pos2, out):
     nc = tc.nc
 
-    def interleave(grouped, raw, lo, hi, copy):
-        if lo < hi:
-            copy(
-                out=grouped[:, lo:hi, :].rearrange("p (c i) t -> p c t i", i=4),
-                in_=raw[:, :, lo:hi].rearrange("p t (c i) -> p c t i", i=4),
-            )
-
     with ExitStack() as ctx:
         keep = ctx.enter_context(tc.tile_pool(name="keep", bufs=1))
+        turns = ctx.enter_context(tc.tile_pool(name="turns", bufs=1))
         psum = ctx.enter_context(tc.psum_pool(name="psum", bufs=1))
 
         offs_tile = keep.tile([P, SLOTS // 16], U16, name="offs_tile")
@@ -61,111 +43,213 @@ def tile_routed_moe_kernel(tc, xT, w, b, gate, offs, pos1, pos2, out):
         bias = keep.tile([P, E], F32, name="bias")
         gate1 = keep.tile([P, T], F32, name="gate1")
         gate2 = keep.tile([P, T], F32, name="gate2")
+        x_scales = keep.tile([P, WINDOW], U8, name="x_scales", align_bytes=64)
+        x_words = keep.tile([P, (A - 1) * T + WINDOW], U32, name="x_words", align_bytes=64)
+        sums = [psum.tile([N, C], F32, name=f"sums_{e}") for e in range(E)]
 
         x_rows = xT.rearrange("(a p t) n -> a p t n", p=P, t=PACK)
-        x_raw = []
-        for a in range(A):
-            for lo, hi, vector_tokens in X_LOADS[a]:
-                raw = keep.tile([P, PACK, hi - lo], F32, name=f"x_raw_{a}_{lo}")
-                nc.sync.dma_start(out=raw[:], in_=x_rows[a][:, :, lo:hi])
-                x_raw.append(raw)
-            if a == 0:
-                nc.sync.dma_start(offs_tile[:], offs)
-        nc.sync.dma_start(out=bias[:], in_=b)
         w_rows = w.flatten_outer_dims().rearrange("(u p t) n -> p u (t n)", p=P, t=PACK)
-        w_raw = []
-        for i, (first, blocks, vector_columns) in enumerate(W_GROUPS):
-            tag = "reused" if i == REUSED_GROUP else f"w_raw_{i}"
-            raw = keep.tile([P, blocks, PACK, N], F32, name=f"w_raw_{i}", tag=tag)
-            nc.sync.dma_start(out=raw[:].rearrange("p u t n -> p u (t n)"), in_=w_rows[:, first : first + blocks, :])
-            w_raw.append(raw)
+        x_raw = {}
+        w_raw = {}
+        w_grouped = {}
+        w_codes = {}
+        slot_words = {}
+        slot_scales = {}
+        results = []
+
+        def place(shape, dtype, name, offset):
+            if offset is None:
+                return keep.tile(shape, dtype, name=name, align_bytes=64)
+            return turns.tile(shape, dtype, name=name, align_bytes=64, offset=offset)
+
+        def load_x(a):
+            raw = keep.tile([P, PACK, T], F32, name=f"x_raw_{a}")
+            nc.sync.dma_start(out=raw[:], in_=x_rows[a])
+            x_raw.update({a: raw})
+
+        def load_w(first, count, step=1, at=None):
+            raw = place([P, count, PACK, N], F32, f"w_raw_{first}", at)
+            rows = w_rows[:, first : first + (count - 1) * step + 1 : step, :]
+            nc.sync.dma_start(out=raw[:].rearrange("p u t n -> p u (t n)"), in_=rows)
+            for j in range(count):
+                w_raw.update({first + j * step: (raw, j)})
+
+        def quantise_x(a, vector_tokens, at=None):
+            grouped = place([P, T, PACK], BF16, f"x_grouped_{a}", at)
+            for copy, lo, hi in ((nc.vector.tensor_copy, 0, vector_tokens), (nc.scalar.copy, vector_tokens, T)):
+                if lo < hi:
+                    copy(
+                        out=grouped[:, lo:hi, :].rearrange("p (c i) t -> p c t i", i=4),
+                        in_=x_raw[a][:, :, lo:hi].rearrange("p t (c i) -> p c t i", i=4),
+                    )
+            start = (A - 1 - a) * T
+            nc.vector.quantize_mx(
+                out=x_words[:, start : start + T].bitcast(FP8X4),
+                scales=x_scales[SCALE_ROW * a : P, 0:T],
+                in_=grouped[:].rearrange("p n t -> p (n t)"),
+            )
+
+        def gather_words(a, lo, hi, at=None):
+            words = place([P, (hi - lo) * C], U32, f"slot_words_{a}_{lo}", at)
+            start = (A - 1 - a) * T
+            window = x_words[:, start : start + WINDOW]
+            nc.vector.tensor_copy(words[:], window.indirect(offs_tile[:, lo * C // 16 : hi * C // 16]))
+            for e in range(lo, hi):
+                slot_words.update({(e, a): words[:, (e - lo) * C : (e - lo + 1) * C]})
+
+        def gather_scales(lo, hi, at=None):
+            scales = place([P, (hi - lo) * C], U8, f"slot_scales_{lo}", at)
+            nc.vector.tensor_copy(scales[:], x_scales[:].indirect(offs_tile[:, lo * C // 16 : hi * C // 16]))
+            for e in range(lo, hi):
+                slot_scales.update({e: (scales, (e - lo) * C)})
+
+        def group(blocks, at=None):
+            grouped = place([P, len(blocks), N, PACK], BF16, f"w_grouped_{blocks[0]}", at)
+            for j, block in enumerate(blocks):
+                w_grouped.update({block: (grouped, j)})
+
+        def interleave(copy, first, count, lo=0, hi=N):
+            raw, i = w_raw[first]
+            grouped, j = w_grouped[first]
+            if count == 1:
+                copy(
+                    out=grouped[:, j, lo:hi].rearrange("p (c i) t -> p c t i", i=4),
+                    in_=raw[:, i, :, lo:hi].rearrange("p t (c i) -> p c t i", i=4),
+                )
+            else:
+                copy(
+                    out=grouped[:, j : j + count].rearrange("p u (c i) t -> p u c t i", i=4),
+                    in_=raw[:, i : i + count].rearrange("p u t (c i) -> p u c t i", i=4),
+                )
+
+        def interleave_gpsimd(first, count):
+            raw, i = w_raw[first]
+            grouped, j = w_grouped[first]
+            nc.gpsimd.tensor_scalar(
+                grouped[:, j : j + count], raw[:, i : i + count].rearrange("p u t n -> p u n t"), 1.0, 0.0, MULT, ADD
+            )
+
+        def quantise_w(blocks, at=None):
+            grouped, j = w_grouped[blocks[0]]
+            width = len(blocks) * N
+            words = place([P, width], U32, f"w_words_{blocks[0]}", at)
+            scales = keep.tile([P, width], U8, name=f"w_scales_{blocks[0]}", align_bytes=64)
+            nc.vector.quantize_mx(
+                out=words[:].bitcast(FP8X4),
+                scales=scales[:],
+                in_=grouped[:, j : j + len(blocks)].rearrange("p u n t -> p (u n t)"),
+            )
+            for i, block in enumerate(blocks):
+                w_codes.update({block: (words[:, i * N : (i + 1) * N], scales[:, i * N : (i + 1) * N])})
+
+        started = []
+
+        def multiply(blocks):
+            for block in blocks:
+                e, a = divmod(block, A)
+                words, scales = w_codes[block]
+                token_scales, first = slot_scales[e]
+                done = len([other for other in started if other // A == e])
+                started.append(block)
+                nc.tensor.matmul_mx(
+                    out=sums[e][:],
+                    lhsT=words.bitcast(FP8X4),
+                    lhsT_scale=scales,
+                    rhs=slot_words[(e, a)].bitcast(FP8X4),
+                    rhs_scale=token_scales[SCALE_ROW * a : P, first : first + C],
+                    start=(done == 0),
+                    stop=(done == A - 1),
+                )
+
+        def relu_scalar(e):
+            nc.scalar.activation(results[0][:, e * C : (e + 1) * C], sums[e][:], RELU, bias=bias[:, e : e + 1])
+
+        def relu_vector(e):
+            nc.vector.tensor_scalar(results[0][:, e * C : (e + 1) * C], sums[e][:], bias[:, e : e + 1], 0.0, ADD, MAX)
+
+        def make_results(at=None):
+            tile = place([P, SLOTS], F32, "results", at)
+            results.append(tile)
+
+        on_scalar = nc.scalar.copy
+        on_vector = nc.vector.tensor_copy
+
+        load_x(0)
+        nc.sync.dma_start(offs_tile[:], offs)
+        load_x(1)
+        load_x(2)
+        nc.sync.dma_start(out=bias[:], in_=b)
+        for first in range(0, 22, 2):
+            load_w(first, 2, at={12: 0, 16: 12288}.get(first))
+        load_w(22, 1)
+        load_w(23, 1)
         nc.sync.dma_start(pos1_tile[:], pos1)
         nc.sync.dma_start(out=gate1[:], in_=gate[0])
         nc.sync.dma_start(pos2_tile[:], pos2)
         nc.sync.dma_start(out=gate2[:], in_=gate[1])
-
-        x_scales = keep.tile([P, WINDOW], U8, name="x_scales", align_bytes=64)
         nc.vector.memset(x_scales[:].bitcast(I32), 0)
-        x_words = keep.tile([P, (A - 1) * T + WINDOW], U32, name="x_words", align_bytes=64)
         nc.vector.memset(x_words[:, A * T :].bitcast(I32), 0)
-
-        slot_words = keep.tile([P, A, SLOTS], U32, name="slot_words", align_bytes=64)
-        slot_scales = keep.tile([P, SLOTS], U8, name="slot_scales", align_bytes=64)
-        piece = 0
-        for a in range(A):
-            grouped = keep.tile([P, T, PACK], BF16, name=f"x_grouped_{a}", align_bytes=64)
-            for lo, hi, vector_tokens in X_LOADS[a]:
-                interleave(grouped[:, lo:hi, :], x_raw[piece], 0, vector_tokens, nc.vector.tensor_copy)
-                interleave(grouped[:, lo:hi, :], x_raw[piece], vector_tokens, hi - lo, nc.scalar.copy)
-                piece += 1
-            start = (A - 1 - a) * T
-            for lo, hi in X_QUANT[a]:
-                nc.vector.quantize_mx(
-                    out=x_words[:, start + lo : start + hi].bitcast(FP8X4),
-                    scales=x_scales[SCALE_ROW * a : P, lo:hi],
-                    in_=grouped[:, lo:hi, :].rearrange("p n t -> p (n t)"),
-                )
-            nc.vector.tensor_copy(slot_words[:, a, :], x_words[:, start : start + WINDOW].indirect(offs_tile[:]))
-        nc.vector.tensor_copy(slot_scales[:], x_scales[:].indirect(offs_tile[:]))
-
-        sums = [psum.tile([N, C], F32, name=f"sums_{e}") for e in range(E)]
-        load = 0
-        for i, blocks in enumerate(W_QUANT):
-            grouped = keep.tile([P, blocks, N, PACK], BF16, name=f"w_grouped_{i}", align_bytes=64)
-            filled = 0
-            members = []
-            while filled < blocks:
-                first, loaded, vector_columns = W_GROUPS[load]
-                target = grouped[:, filled : filled + loaded]
-                if loaded == 1:
-                    interleave(target[:, 0], w_raw[load][:, 0], 0, N - vector_columns, nc.scalar.copy)
-                    interleave(target[:, 0], w_raw[load][:, 0], N - vector_columns, N, nc.vector.tensor_copy)
-                else:
-                    split = loaded - vector_columns // N
-                    for copy, lo, hi in ((nc.scalar.copy, 0, split), (nc.vector.tensor_copy, split, loaded)):
-                        if lo < hi:
-                            copy(
-                                out=target[:, lo:hi].rearrange("p u (c i) t -> p u c t i", i=4),
-                                in_=w_raw[load][:, lo:hi].rearrange("p u t (c i) -> p u c t i", i=4),
-                            )
-                members.extend(range(first, first + loaded))
-                filled += loaded
-                load += 1
-            w_words = keep.tile([P, blocks * N], U32, name=f"w_words_{i}", align_bytes=64)
-            w_scales = keep.tile([P, blocks * N], U8, name=f"w_scales_{i}", align_bytes=64)
-            nc.vector.quantize_mx(
-                out=w_words[:].bitcast(FP8X4),
-                scales=w_scales[:],
-                in_=grouped[:].rearrange("p u n t -> p (u n t)"),
-            )
-            for j, block in enumerate(members):
-                e, a = divmod(block, A)
-                features = slice(j * N, (j + 1) * N)
-                places = slice(e * C, (e + 1) * C)
-                nc.tensor.matmul_mx(
-                    out=sums[e][:],
-                    lhsT=w_words[:, features].bitcast(FP8X4),
-                    lhsT_scale=w_scales[:, features],
-                    rhs=slot_words[:, a, places].bitcast(FP8X4),
-                    rhs_scale=slot_scales[SCALE_ROW * a : P, places],
-                    start=(a == 0),
-                    stop=(a == A - 1),
-                )
-
-        results = keep.tile([P, SLOTS], F32, name="results", tag="reused")
-        for e in range(E):
-            places = slice(e * C, (e + 1) * C)
-            if e in VECTOR_RELUS:
-                nc.vector.tensor_scalar(results[:, places], sums[e][:], bias[:, e : e + 1], 0.0, ADD, MAX)
-            else:
-                nc.scalar.activation(results[:, places], sums[e][:], RELU, bias=bias[:, e : e + 1])
+        quantise_x(0, 320)
+        gather_words(0, 0, 8)
+        quantise_x(1, 0)
+        gather_words(1, 0, 8)
+        quantise_x(2, 0)
+        gather_words(2, 0, 4)
+        gather_scales(0, 4)
+        group((0, 1))
+        interleave_gpsimd(0, 2)
+        quantise_w((0, 1))
+        for first in (2, 6):
+            group((first, first + 1, first + 2, first + 3))
+            interleave(on_scalar, first, 2)
+            interleave(on_scalar, first + 2, 2)
+            quantise_w((first, first + 1, first + 2, first + 3))
+        group((10, 11), at=4096 + 1024)
+        interleave(on_scalar, 10, 2)
+        quantise_w((10, 11))
+        multiply(range(12))
+        gather_words(2, 4, 8, at=4096 - 0)
+        gather_scales(4, 8, at=4096 + 2048)
+        group((14, 15), at=4096 + 2560)
+        interleave_gpsimd(14, 2)
+        group((12, 13))
+        interleave(on_scalar, 12, 2)
+        make_results(at=0)
+        for e in range(4):
+            relu_scalar(e)
+        quantise_w((12, 13))
+        group((16, 17))
+        interleave(on_scalar, 16, 2)
+        quantise_w((14, 15), at=12288)
+        quantise_w((16, 17))
+        multiply(range(12, 18))
+        group((18, 19))
+        interleave(on_scalar, 18, 2)
+        group((20, 21))
+        interleave(on_vector, 20, 2)
+        quantise_w((18, 19))
+        quantise_w((20, 21))
+        multiply(range(18, 22))
+        for e in (4, 5):
+            relu_scalar(e)
+        group((22,))
+        interleave(on_scalar, 22, 1)
+        group((23,))
+        interleave(on_vector, 23, 1, 64, 128)
+        interleave(on_scalar, 23, 1, 0, 64)
+        quantise_w((22,))
+        multiply((22,))
+        quantise_w((23,))
+        multiply((23,))
+        relu_vector(6)
+        relu_scalar(7)
 
         y1 = keep.tile([P, T], F32, name="y1")
-        nc.vector.tensor_tensor(y1[:], results[:].indirect(pos1_tile[:]), gate1[:], MULT)
+        nc.vector.tensor_tensor(y1[:], results[0][:].indirect(pos1_tile[:]), gate1[:], MULT)
         y2 = []
         for lo, hi in OUT_CUTS:
             part = keep.tile([P, hi - lo], F32, name=f"y2_{lo}")
-            nc.vector.tensor_tensor(part[:], results[:].indirect(pos2_tile[:, lo // 16 : hi // 16]), gate2[:, lo:hi], MULT)
+            nc.vector.tensor_tensor(part[:], results[0][:].indirect(pos2_tile[:, lo // 16 : hi // 16]), gate2[:, lo:hi], MULT)
             y2.append(part)
         for (lo, hi), part in zip(OUT_CUTS, y2):
             y = keep.tile([P, hi - lo], F32, name=f"y_{lo}")

@@ -74,14 +74,18 @@ def tile_routed_moe_kernel(tc, xT, w, b, gate, offs, pos1, pos2, out):
             for j in range(count):
                 w_raw.update({first + j * step: (raw, j)})
 
-        def quantise_x(a, vector_tokens, at=None):
-            grouped = place([P, T, PACK], BF16, f"x_grouped_{a}", at)
-            for copy, lo, hi in ((nc.vector.tensor_copy, 0, vector_tokens), (nc.scalar.copy, vector_tokens, T)):
-                if lo < hi:
-                    copy(
-                        out=grouped[:, lo:hi, :].rearrange("p (c i) t -> p c t i", i=4),
-                        in_=x_raw[a][:, :, lo:hi].rearrange("p t (c i) -> p c t i", i=4),
-                    )
+        x_grouped = {}
+
+        def interleave_x(copy, a, lo, hi, at=None):
+            if a not in x_grouped:
+                x_grouped.update({a: place([P, T, PACK], BF16, f"x_grouped_{a}", at)})
+            copy(
+                out=x_grouped[a][:, lo:hi, :].rearrange("p (c i) t -> p c t i", i=4),
+                in_=x_raw[a][:, :, lo:hi].rearrange("p t (c i) -> p c t i", i=4),
+            )
+
+        def quantise_x(a):
+            grouped = x_grouped[a]
             start = (A - 1 - a) * T
             nc.vector.quantize_mx(
                 out=x_words[:, start : start + T].bitcast(FP8X4),
@@ -174,13 +178,17 @@ def tile_routed_moe_kernel(tc, xT, w, b, gate, offs, pos1, pos2, out):
         on_scalar = nc.scalar.copy
         on_vector = nc.vector.tensor_copy
 
+        def scalar_pair(first, at=None):
+            group((first, first + 1), at)
+            interleave(on_scalar, first, 2)
+
         load_x(0)
         nc.sync.dma_start(offs_tile[:], offs)
         load_x(1)
         load_x(2)
         nc.sync.dma_start(out=bias[:], in_=b)
         for first in range(0, 22, 2):
-            load_w(first, 2, at={12: 0, 16: 12288}.get(first))
+            load_w(first, 2, at={0: 1024, 14: 8192}.get(first))
         load_w(22, 1)
         load_w(23, 1)
         nc.sync.dma_start(pos1_tile[:], pos1)
@@ -189,48 +197,43 @@ def tile_routed_moe_kernel(tc, xT, w, b, gate, offs, pos1, pos2, out):
         nc.sync.dma_start(out=gate2[:], in_=gate[1])
         nc.vector.memset(x_scales[:].bitcast(I32), 0)
         nc.vector.memset(x_words[:, A * T :].bitcast(I32), 0)
-        quantise_x(0, 320)
+        interleave_x(on_vector, 0, 0, 320)
+        interleave_x(on_scalar, 0, 320, 512)
+        quantise_x(0)
         gather_words(0, 0, 8)
-        quantise_x(1, 0)
+        interleave_x(on_scalar, 1, 0, 512)
+        quantise_x(1)
+        interleave_x(on_vector, 2, 0, 128)
+        interleave_x(on_scalar, 2, 128, 512)
         gather_words(1, 0, 8)
-        quantise_x(2, 0)
-        gather_words(2, 0, 4)
-        gather_scales(0, 4)
-        group((0, 1))
-        interleave_gpsimd(0, 2)
+        quantise_x(2)
+        scalar_pair(0)
         quantise_w((0, 1))
-        for first in (2, 6):
+        gather_words(2, 0, 8, at=0)
+        gather_scales(0, 8, at=4096)
+        for first in (2, 6, 10):
             group((first, first + 1, first + 2, first + 3))
             interleave(on_scalar, first, 2)
             interleave(on_scalar, first + 2, 2)
-            quantise_w((first, first + 1, first + 2, first + 3))
-        group((10, 11), at=4096 + 1024)
-        interleave(on_scalar, 10, 2)
-        quantise_w((10, 11))
-        multiply(range(12))
-        gather_words(2, 4, 8, at=4096 - 0)
-        gather_scales(4, 8, at=4096 + 2048)
-        group((14, 15), at=4096 + 2560)
-        interleave_gpsimd(14, 2)
-        group((12, 13))
-        interleave(on_scalar, 12, 2)
-        make_results(at=0)
-        for e in range(4):
+            if first < 10:
+                quantise_w((first, first + 1, first + 2, first + 3))
+        multiply(range(10))
+        group((14, 15, 16, 17))
+        interleave(on_scalar, 14, 2)
+        make_results(at=6144)
+        for e in range(3):
             relu_scalar(e)
-        quantise_w((12, 13))
-        group((16, 17))
-        interleave(on_scalar, 16, 2)
-        quantise_w((14, 15), at=12288)
-        quantise_w((16, 17))
-        multiply(range(12, 18))
-        group((18, 19))
-        interleave(on_scalar, 18, 2)
+        interleave(on_vector, 16, 2)
+        quantise_w((10, 11, 12, 13), at=10240)
+        quantise_w((14, 15, 16, 17))
+        multiply(range(10, 18))
+        scalar_pair(18)
         group((20, 21))
         interleave(on_vector, 20, 2)
         quantise_w((18, 19))
         quantise_w((20, 21))
         multiply(range(18, 22))
-        for e in (4, 5):
+        for e in (3, 4, 5):
             relu_scalar(e)
         group((22,))
         interleave(on_scalar, 22, 1)

@@ -26,7 +26,7 @@ WINDOW = 1408
 
 SCALE_ROW = 4
 
-OUT_CUTS = ((0, 320), (320, 512))
+OUT_CUTS = ((0, 256), (256, 512))
 
 
 def tile_routed_moe_kernel(tc, xT, w, b, gate, offs, pos1, pos2, out):
@@ -62,15 +62,15 @@ def tile_routed_moe_kernel(tc, xT, w, b, gate, offs, pos1, pos2, out):
                 return keep.tile(shape, dtype, name=name, align_bytes=64)
             return turns.tile(shape, dtype, name=name, align_bytes=64, offset=offset)
 
-        def load_x(a):
-            raw = keep.tile([P, PACK, T], F32, name=f"x_raw_{a}")
+        def load_x(a, at=None):
+            raw = place([P, PACK, T], F32, f"x_raw_{a}", at)
             nc.sync.dma_start(out=raw[:], in_=x_rows[a])
             x_raw.update({a: raw})
 
-        def load_w(first, count, step=1, at=None):
+        def load_w(first, count, step=1, at=None, queue=nc.sync):
             raw = place([P, count, PACK, N], F32, f"w_raw_{first}", at)
             rows = w_rows[:, first : first + (count - 1) * step + 1 : step, :]
-            nc.sync.dma_start(out=raw[:].rearrange("p u t n -> p u (t n)"), in_=rows)
+            queue.dma_start(out=raw[:].rearrange("p u t n -> p u (t n)"), in_=rows)
             for j in range(count):
                 w_raw.update({first + j * step: (raw, j)})
 
@@ -238,8 +238,8 @@ def tile_routed_moe_kernel(tc, xT, w, b, gate, offs, pos1, pos2, out):
         group((22,))
         interleave(on_scalar, 22, 1)
         group((23,))
-        interleave(on_vector, 23, 1, 64, 128)
-        interleave(on_scalar, 23, 1, 0, 64)
+        interleave(on_vector, 23, 1, 32, 128)
+        interleave(on_scalar, 23, 1, 0, 32)
         quantise_w((22,))
         multiply((22,))
         quantise_w((23,))

@@ -244,7 +244,7 @@ def tile_routed_moe_kernel(tc, xT, w, b, gate, offs, pos1, pos2, out):
         multiply((22,))
         quantise_w((23,))
         multiply((23,))
-        relu_vector(6)
+        relu_scalar(6)
         relu_scalar(7)
 
         y1 = keep.tile([P, T], F32, name="y1")

@@ -19,14 +19,13 @@ U8 = mybir.dt.uint8
 FP8X4 = mybir.dt.float8_e4m3fn_x4
 RELU = mybir.ActivationFunctionType.Relu
 ADD = mybir.AluOpType.add
-MAX = mybir.AluOpType.max
 MULT = mybir.AluOpType.mult
 
 WINDOW = 1408
 
 SCALE_ROW = 4
 
-OUT_CUTS = ((0, 256), (256, 512))
+KIB = 1024
 
 
 def tile_routed_moe_kernel(tc, xT, w, b, gate, offs, pos1, pos2, out):
@@ -49,138 +48,122 @@ def tile_routed_moe_kernel(tc, xT, w, b, gate, offs, pos1, pos2, out):
 
         x_rows = xT.rearrange("(a p t) n -> a p t n", p=P, t=PACK)
         w_rows = w.flatten_outer_dims().rearrange("(u p t) n -> p u (t n)", p=P, t=PACK)
-        x_raw = {}
-        w_raw = {}
-        w_grouped = {}
-        w_codes = {}
-        slot_words = {}
-        slot_scales = {}
-        results = []
+        x_raw, x_grouped, slot_words = {}, {}, {}
+        w_raw, w_grouped, w_codes = {}, {}, {}
+        held = {}
+        multiplied = []
 
-        def place(shape, dtype, name, offset):
-            if offset is None:
+        def place(shape, dtype, name, at=None):
+            if at is None:
                 return keep.tile(shape, dtype, name=name, align_bytes=64)
-            return turns.tile(shape, dtype, name=name, align_bytes=64, offset=offset)
+            return turns.tile(shape, dtype, name=name, align_bytes=64, offset=at)
 
         def load_x(a, at=None):
             raw = place([P, PACK, T], F32, f"x_raw_{a}", at)
             nc.sync.dma_start(out=raw[:], in_=x_rows[a])
             x_raw.update({a: raw})
 
-        def load_w(first, count, step=1, at=None, queue=nc.sync):
+        def load_w(first, count, at=None):
             raw = place([P, count, PACK, N], F32, f"w_raw_{first}", at)
-            rows = w_rows[:, first : first + (count - 1) * step + 1 : step, :]
-            queue.dma_start(out=raw[:].rearrange("p u t n -> p u (t n)"), in_=rows)
+            nc.sync.dma_start(out=raw[:].rearrange("p u t n -> p u (t n)"), in_=w_rows[:, first : first + count, :])
             for j in range(count):
-                w_raw.update({first + j * step: (raw, j)})
+                w_raw.update({first + j: (raw, j)})
 
-        x_grouped = {}
+        def group_x(a, at=None):
+            x_grouped.update({a: place([P, T, PACK], BF16, f"x_grouped_{a}", at)})
 
-        def interleave_x(copy, a, lo, hi, at=None):
-            if a not in x_grouped:
-                x_grouped.update({a: place([P, T, PACK], BF16, f"x_grouped_{a}", at)})
+        def interleave_x(copy, a, lo, hi):
             copy(
                 out=x_grouped[a][:, lo:hi, :].rearrange("p (c i) t -> p c t i", i=4),
                 in_=x_raw[a][:, :, lo:hi].rearrange("p t (c i) -> p c t i", i=4),
             )
 
-        def quantise_x(a):
-            grouped = x_grouped[a]
+        def quantise_x(a, lo=0, hi=T):
             start = (A - 1 - a) * T
             nc.vector.quantize_mx(
-                out=x_words[:, start : start + T].bitcast(FP8X4),
-                scales=x_scales[SCALE_ROW * a : P, 0:T],
-                in_=grouped[:].rearrange("p n t -> p (n t)"),
+                out=x_words[:, start + lo : start + hi].bitcast(FP8X4),
+                scales=x_scales[SCALE_ROW * a : P, lo:hi],
+                in_=x_grouped[a][:, lo:hi, :].rearrange("p n t -> p (n t)"),
             )
 
-        def gather_words(a, lo, hi, at=None):
-            words = place([P, (hi - lo) * C], U32, f"slot_words_{a}_{lo}", at)
+        def gather_words(a, at=None):
+            words = place([P, SLOTS], U32, f"slot_words_{a}", at)
             start = (A - 1 - a) * T
-            window = x_words[:, start : start + WINDOW]
-            nc.vector.tensor_copy(words[:], window.indirect(offs_tile[:, lo * C // 16 : hi * C // 16]))
-            for e in range(lo, hi):
-                slot_words.update({(e, a): words[:, (e - lo) * C : (e - lo + 1) * C]})
+            nc.vector.tensor_copy(words[:], x_words[:, start : start + WINDOW].indirect(offs_tile[:]))
+            slot_words.update({a: words})
 
-        def gather_scales(lo, hi, at=None):
-            scales = place([P, (hi - lo) * C], U8, f"slot_scales_{lo}", at)
-            nc.vector.tensor_copy(scales[:], x_scales[:].indirect(offs_tile[:, lo * C // 16 : hi * C // 16]))
-            for e in range(lo, hi):
-                slot_scales.update({e: (scales, (e - lo) * C)})
+        def gather_scales(at=None):
+            scales = place([P, SLOTS], U8, "slot_scales", at)
+            nc.vector.tensor_copy(scales[:], x_scales[:].indirect(offs_tile[:]))
+            held.update({"slot_scales": scales})
 
-        def group(blocks, at=None):
-            grouped = place([P, len(blocks), N, PACK], BF16, f"w_grouped_{blocks[0]}", at)
-            for j, block in enumerate(blocks):
-                w_grouped.update({block: (grouped, j)})
+        def group(name, count, at=None):
+            return place([P, count, N, PACK], BF16, name, at)
 
-        def interleave(copy, first, count, lo=0, hi=N):
+        def seat(tile, pieces, first=0):
+            for j, piece in enumerate(pieces):
+                w_grouped.update({piece: (tile, first + j)})
+
+        def interleave(copy, first, count):
             raw, i = w_raw[first]
             grouped, j = w_grouped[first]
-            if count == 1:
-                copy(
-                    out=grouped[:, j, lo:hi].rearrange("p (c i) t -> p c t i", i=4),
-                    in_=raw[:, i, :, lo:hi].rearrange("p t (c i) -> p c t i", i=4),
-                )
-            else:
-                copy(
-                    out=grouped[:, j : j + count].rearrange("p u (c i) t -> p u c t i", i=4),
-                    in_=raw[:, i : i + count].rearrange("p u t (c i) -> p u c t i", i=4),
-                )
-
-        def interleave_gpsimd(first, count):
-            raw, i = w_raw[first]
-            grouped, j = w_grouped[first]
-            nc.gpsimd.tensor_scalar(
-                grouped[:, j : j + count], raw[:, i : i + count].rearrange("p u t n -> p u n t"), 1.0, 0.0, MULT, ADD
+            copy(
+                out=grouped[:, j : j + count].rearrange("p u (c i) t -> p u c t i", i=4),
+                in_=raw[:, i : i + count].rearrange("p u t (c i) -> p u c t i", i=4),
             )
 
-        def quantise_w(blocks, at=None):
-            grouped, j = w_grouped[blocks[0]]
-            width = len(blocks) * N
-            words = place([P, width], U32, f"w_words_{blocks[0]}", at)
-            scales = keep.tile([P, width], U8, name=f"w_scales_{blocks[0]}", align_bytes=64)
+        def interleave_part(copy, piece, lo=0, hi=N):
+            raw, i = w_raw[piece]
+            grouped, j = w_grouped[piece]
+            copy(
+                out=grouped[:, j, lo:hi].rearrange("p (c i) t -> p c t i", i=4),
+                in_=raw[:, i, :, lo:hi].rearrange("p t (c i) -> p c t i", i=4),
+            )
+
+        def quantise_w(pieces, at=None):
+            grouped, j = w_grouped[pieces[0]]
+            width = len(pieces) * N
+            words = place([P, width], U32, f"w_words_{pieces[0]}", at)
+            scales = keep.tile([P, width], U8, name=f"w_scales_{pieces[0]}", align_bytes=64)
             nc.vector.quantize_mx(
                 out=words[:].bitcast(FP8X4),
                 scales=scales[:],
-                in_=grouped[:, j : j + len(blocks)].rearrange("p u n t -> p (u n t)"),
+                in_=grouped[:, j : j + len(pieces)].rearrange("p u n t -> p (u n t)"),
             )
-            for i, block in enumerate(blocks):
-                w_codes.update({block: (words[:, i * N : (i + 1) * N], scales[:, i * N : (i + 1) * N])})
+            for i, piece in enumerate(pieces):
+                w_codes.update({piece: (words[:, i * N : (i + 1) * N], scales[:, i * N : (i + 1) * N])})
 
-        started = []
-
-        def multiply(blocks):
-            for block in blocks:
-                e, a = divmod(block, A)
-                words, scales = w_codes[block]
-                token_scales, first = slot_scales[e]
-                done = len([other for other in started if other // A == e])
-                started.append(block)
+        def multiply(pieces):
+            for piece in pieces:
+                e, a = divmod(piece, A)
+                words, scales = w_codes[piece]
+                done = len([other for other in multiplied if other // A == e])
+                multiplied.append(piece)
                 nc.tensor.matmul_mx(
                     out=sums[e][:],
                     lhsT=words.bitcast(FP8X4),
                     lhsT_scale=scales,
-                    rhs=slot_words[(e, a)].bitcast(FP8X4),
-                    rhs_scale=token_scales[SCALE_ROW * a : P, first : first + C],
+                    rhs=slot_words[a][:, e * C : (e + 1) * C].bitcast(FP8X4),
+                    rhs_scale=held["slot_scales"][SCALE_ROW * a : P, e * C : (e + 1) * C],
                     start=(done == 0),
                     stop=(done == A - 1),
                 )
 
-        def relu_scalar(e):
-            nc.scalar.activation(results[0][:, e * C : (e + 1) * C], sums[e][:], RELU, bias=bias[:, e : e + 1])
-
-        def relu_vector(e):
-            nc.vector.tensor_scalar(results[0][:, e * C : (e + 1) * C], sums[e][:], bias[:, e : e + 1], 0.0, ADD, MAX)
+        def relu(experts):
+            for e in experts:
+                nc.scalar.activation(held["results"][:, e * C : (e + 1) * C], sums[e][:], RELU, bias=bias[:, e : e + 1])
 
         def make_results(at=None):
-            tile = place([P, SLOTS], F32, "results", at)
-            results.append(tile)
+            held.update({"results": place([P, SLOTS], F32, "results", at)})
+
+        def load_way_back():
+            nc.sync.dma_start(pos1_tile[:], pos1)
+            nc.sync.dma_start(out=gate1[:], in_=gate[0])
+            nc.sync.dma_start(pos2_tile[:], pos2)
+            nc.sync.dma_start(out=gate2[:], in_=gate[1])
 
         on_scalar = nc.scalar.copy
         on_vector = nc.vector.tensor_copy
-
-        def scalar_pair(first, at=None):
-            group((first, first + 1), at)
-            interleave(on_scalar, first, 2)
 
         load_x(0)
         nc.sync.dma_start(offs_tile[:], offs)
@@ -188,73 +171,80 @@ def tile_routed_moe_kernel(tc, xT, w, b, gate, offs, pos1, pos2, out):
         load_x(2)
         nc.sync.dma_start(out=bias[:], in_=b)
         for first in range(0, 22, 2):
-            load_w(first, 2, at={0: 1024, 14: 8192}.get(first))
+            load_w(first, 2, at={0: 1 * KIB, 14: 8 * KIB}.get(first))
         load_w(22, 1)
         load_w(23, 1)
-        nc.sync.dma_start(pos1_tile[:], pos1)
-        nc.sync.dma_start(out=gate1[:], in_=gate[0])
-        nc.sync.dma_start(pos2_tile[:], pos2)
-        nc.sync.dma_start(out=gate2[:], in_=gate[1])
+        load_way_back()
+
         nc.vector.memset(x_scales[:].bitcast(I32), 0)
         nc.vector.memset(x_words[:, A * T :].bitcast(I32), 0)
-        interleave_x(on_vector, 0, 0, 320)
-        interleave_x(on_scalar, 0, 320, 512)
-        quantise_x(0)
-        gather_words(0, 0, 8)
-        interleave_x(on_scalar, 1, 0, 512)
-        quantise_x(1)
+        group_x(0)
+        interleave_x(on_vector, 0, 0, 256)
+        interleave_x(on_vector, 0, 256, 352)
+        interleave_x(on_scalar, 0, 352, T)
+        quantise_x(0, 0, 256)
+        quantise_x(0, 256, T)
+        gather_words(0)
+        group_x(1)
+        interleave_x(on_scalar, 1, 256, T)
+        interleave_x(on_scalar, 1, 128, 256)
+        interleave_x(on_vector, 1, 0, 128)
+        quantise_x(1, 256, T)
+        quantise_x(1, 0, 256)
+        group_x(2)
         interleave_x(on_vector, 2, 0, 128)
-        interleave_x(on_scalar, 2, 128, 512)
-        gather_words(1, 0, 8)
+        interleave_x(on_scalar, 2, 128, T)
+        gather_words(1)
         quantise_x(2)
-        scalar_pair(0)
+        seat(group("g0", 2), (0, 1))
+        interleave(on_scalar, 0, 2)
         quantise_w((0, 1))
-        gather_words(2, 0, 8, at=0)
-        gather_scales(0, 8, at=4096)
+        gather_words(2, at=0)
+        gather_scales(at=4 * KIB)
         for first in (2, 6, 10):
-            group((first, first + 1, first + 2, first + 3))
+            seat(group(f"g{first}", 4), range(first, first + 4))
             interleave(on_scalar, first, 2)
             interleave(on_scalar, first + 2, 2)
             if first < 10:
-                quantise_w((first, first + 1, first + 2, first + 3))
+                quantise_w(range(first, first + 4))
         multiply(range(10))
-        group((14, 15, 16, 17))
+        seat(group("g14", 4), range(14, 18))
         interleave(on_scalar, 14, 2)
-        make_results(at=6144)
-        for e in range(3):
-            relu_scalar(e)
+        make_results(at=6 * KIB)
+        relu(range(3))
         interleave(on_vector, 16, 2)
-        quantise_w((10, 11, 12, 13), at=10240)
+        quantise_w((10, 11, 12, 13), at=10 * KIB)
         quantise_w((14, 15, 16, 17))
         multiply(range(10, 18))
-        scalar_pair(18)
-        group((20, 21))
+        seat(group("g18", 2), (18, 19))
+        interleave(on_scalar, 18, 2)
+        seat(group("g20", 2), (20, 21))
         interleave(on_vector, 20, 2)
         quantise_w((18, 19))
         quantise_w((20, 21))
         multiply(range(18, 22))
-        for e in (3, 4, 5):
-            relu_scalar(e)
-        group((22,))
-        interleave(on_scalar, 22, 1)
-        group((23,))
-        interleave(on_vector, 23, 1, 32, 128)
-        interleave(on_scalar, 23, 1, 0, 32)
+        relu((3, 4, 5))
+        seat(group("g22", 1), (22,))
+        interleave_part(on_scalar, 22)
+        seat(group("g23", 1), (23,))
+        interleave_part(on_vector, 23, 32, N)
+        interleave_part(on_scalar, 23, 0, 32)
         quantise_w((22,))
         multiply((22,))
         quantise_w((23,))
         multiply((23,))
-        relu_scalar(6)
-        relu_scalar(7)
+        relu((6, 7))
 
+        results = held["results"]
+        halves = ((0, T // 2), (T // 2, T))
         y1 = keep.tile([P, T], F32, name="y1")
-        nc.vector.tensor_tensor(y1[:], results[0][:].indirect(pos1_tile[:]), gate1[:], MULT)
+        nc.vector.tensor_tensor(y1[:], results[:].indirect(pos1_tile[:]), gate1[:], MULT)
         y2 = []
-        for lo, hi in OUT_CUTS:
+        for lo, hi in halves:
             part = keep.tile([P, hi - lo], F32, name=f"y2_{lo}")
-            nc.vector.tensor_tensor(part[:], results[0][:].indirect(pos2_tile[:, lo // 16 : hi // 16]), gate2[:, lo:hi], MULT)
+            nc.vector.tensor_tensor(part[:], results[:].indirect(pos2_tile[:, lo // 16 : hi // 16]), gate2[:, lo:hi], MULT)
             y2.append(part)
-        for (lo, hi), part in zip(OUT_CUTS, y2):
+        for (lo, hi), part in zip(halves, y2):
             y = keep.tile([P, hi - lo], F32, name=f"y_{lo}")
             nc.vector.tensor_tensor(y[:], y1[:, lo:hi], part[:], ADD)
             nc.sync.dma_start(out=out[:, lo:hi], in_=y[:])

@@ -86,11 +86,13 @@ def tile_routed_moe_kernel(tc, xT, w, b, gate, offs, pos1, pos2, out):
                 in_=x_grouped[a][:, lo:hi, :].rearrange("p n t -> p (n t)"),
             )
 
-        def gather_words(a, at=None):
-            words = place([P, SLOTS], U32, f"slot_words_{a}", at)
+        def gather_words(a, lo=0, hi=E, at=None):
+            words = place([P, (hi - lo) * C], U32, f"slot_words_{a}_{lo}", at)
             start = (A - 1 - a) * T
-            nc.vector.tensor_copy(words[:], x_words[:, start : start + WINDOW].indirect(offs_tile[:]))
-            slot_words.update({a: words})
+            window = x_words[:, start : start + WINDOW]
+            nc.vector.tensor_copy(words[:], window.indirect(offs_tile[:, lo * C // 16 : hi * C // 16]))
+            for e in range(lo, hi):
+                slot_words.update({(a, e): words[:, (e - lo) * C : (e - lo + 1) * C]})
 
         def gather_scales(at=None):
             scales = place([P, SLOTS], U8, "slot_scales", at)
@@ -143,7 +145,7 @@ def tile_routed_moe_kernel(tc, xT, w, b, gate, offs, pos1, pos2, out):
                     out=sums[e][:],
                     lhsT=words.bitcast(FP8X4),
                     lhsT_scale=scales,
-                    rhs=slot_words[a][:, e * C : (e + 1) * C].bitcast(FP8X4),
+                    rhs=slot_words[(a, e)].bitcast(FP8X4),
                     rhs_scale=held["slot_scales"][SCALE_ROW * a : P, e * C : (e + 1) * C],
                     start=(done == 0),
                     stop=(done == A - 1),
@@ -192,8 +194,8 @@ def tile_routed_moe_kernel(tc, xT, w, b, gate, offs, pos1, pos2, out):
         quantise_x(1, 256, T)
         quantise_x(1, 0, 256)
         group_x(2)
-        interleave_x(on_vector, 2, 0, 128)
-        interleave_x(on_scalar, 2, 128, T)
+        interleave_x(on_vector, 2, 0, 256)
+        interleave_x(on_scalar, 2, 256, T)
         gather_words(1)
         quantise_x(2)
         seat(group("g0", 2), (0, 1))
@@ -234,6 +236,7 @@ def tile_routed_moe_kernel(tc, xT, w, b, gate, offs, pos1, pos2, out):
         quantise_w((23,))
         multiply((23,))
         relu((6, 7))
+
 
         results = held["results"]
         halves = ((0, T // 2), (T // 2, T))

@@ -5,8 +5,9 @@ import concourse.mybir as mybir
 K, T, E, C, N = 1536, 512, 8, 128, 128
 P = 128
 PACK = 4
-A = K // (P * PACK)
+PASSES = K // (P * PACK)
 SLOTS = E * C
+LANES = 16
 
 FLOPS = 2 * K * N * SLOTS
 
@@ -18,236 +19,205 @@ U16 = mybir.dt.uint16
 U8 = mybir.dt.uint8
 FP8X4 = mybir.dt.float8_e4m3fn_x4
 RELU = mybir.ActivationFunctionType.Relu
+COPY = mybir.ActivationFunctionType.Copy
 ADD = mybir.AluOpType.add
 MULT = mybir.AluOpType.mult
 
 WINDOW = 1408
-
 SCALE_ROW = 4
-
+RUN = 4
 KIB = 1024
 
 
 def tile_routed_moe_kernel(tc, xT, w, b, gate, offs, pos1, pos2, out):
     nc = tc.nc
+    scalar_copy = nc.scalar.copy
+    vector_copy = nc.vector.tensor_copy
 
     with ExitStack() as ctx:
         keep = ctx.enter_context(tc.tile_pool(name="keep", bufs=1))
-        turns = ctx.enter_context(tc.tile_pool(name="turns", bufs=1))
+        shared = ctx.enter_context(tc.tile_pool(name="shared", bufs=1))
         psum = ctx.enter_context(tc.psum_pool(name="psum", bufs=1))
 
-        offs_tile = keep.tile([P, SLOTS // 16], U16, name="offs_tile")
-        pos1_tile = keep.tile([P, T // 16], U16, name="pos1_tile")
-        pos2_tile = keep.tile([P, T // 16], U16, name="pos2_tile")
-        bias = keep.tile([P, E], F32, name="bias")
-        gate1 = keep.tile([P, T], F32, name="gate1")
-        gate2 = keep.tile([P, T], F32, name="gate2")
-        x_scales = keep.tile([P, WINDOW], U8, name="x_scales", align_bytes=64)
-        x_words = keep.tile([P, (A - 1) * T + WINDOW], U32, name="x_words", align_bytes=64)
+        def tile(shape, dtype, name, at=None):
+            if at is None:
+                return keep.tile(shape, dtype, name=name, align_bytes=64)
+            return shared.tile(shape, dtype, name=name, align_bytes=64, offset=at)
+
+        offs_tile = keep.tile([P, SLOTS // LANES], U16, name="offs_tile")
+        pos1_tile = keep.tile([P, T // LANES], U16, name="pos1_tile")
+        pos2_tile = keep.tile([P, T // LANES], U16, name="pos2_tile")
+        bias = tile([P, E], F32, "bias")
+        gate1 = tile([P, T], F32, "gate1")
+        gate2 = tile([P, T], F32, "gate2")
+        x_scales = tile([P, WINDOW], U8, "x_scales")
+        x_words = tile([P, (PASSES - 1) * T + WINDOW], U32, "x_words")
+        x_raw = [tile([P, PACK, T], F32, f"x_raw_{a}") for a in range(PASSES)]
+        x_grouped = [tile([P, T, PACK], BF16, f"x_grouped_{a}") for a in range(PASSES)]
         sums = [psum.tile([N, C], F32, name=f"sums_{e}") for e in range(E)]
 
         x_rows = xT.rearrange("(a p t) n -> a p t n", p=P, t=PACK)
         w_rows = w.flatten_outer_dims().rearrange("(u p t) n -> p u (t n)", p=P, t=PACK)
-        x_raw, x_grouped, slot_words = {}, {}, {}
-        w_raw, w_grouped, w_codes = {}, {}, {}
-        held = {}
-        multiplied = []
-
-        def place(shape, dtype, name, at=None):
-            if at is None:
-                return keep.tile(shape, dtype, name=name, align_bytes=64)
-            return turns.tile(shape, dtype, name=name, align_bytes=64, offset=at)
-
-        def load_x(a, at=None):
-            raw = place([P, PACK, T], F32, f"x_raw_{a}", at)
-            nc.sync.dma_start(out=raw[:], in_=x_rows[a])
-            x_raw.update({a: raw})
+        w_raw, w_grouped, w_codes, slot_words = {}, {}, {}, {}
 
         def load_w(first, count, at=None):
-            raw = place([P, count, PACK, N], F32, f"w_raw_{first}", at)
+            raw = tile([P, count, PACK, N], F32, f"w_raw_{first}", at)
             nc.sync.dma_start(out=raw[:].rearrange("p u t n -> p u (t n)"), in_=w_rows[:, first : first + count, :])
-            for j in range(count):
-                w_raw.update({first + j: (raw, j)})
-
-        def group_x(a, at=None):
-            x_grouped.update({a: place([P, T, PACK], BF16, f"x_grouped_{a}", at)})
+            w_raw.update({first + j: (raw, j) for j in range(count)})
 
         def interleave_x(copy, a, lo, hi):
             copy(
-                out=x_grouped[a][:, lo:hi, :].rearrange("p (c i) t -> p c t i", i=4),
-                in_=x_raw[a][:, :, lo:hi].rearrange("p t (c i) -> p c t i", i=4),
+                out=x_grouped[a][:, lo:hi, :].rearrange("p (c i) t -> p c t i", i=RUN),
+                in_=x_raw[a][:, :, lo:hi].rearrange("p t (c i) -> p c t i", i=RUN),
             )
 
-        def quantise_x(a, lo=0, hi=T):
-            start = (A - 1 - a) * T
+        def quantise_x(a, lo, hi):
+            start = (PASSES - 1 - a) * T
             nc.vector.quantize_mx(
                 out=x_words[:, start + lo : start + hi].bitcast(FP8X4),
                 scales=x_scales[SCALE_ROW * a : P, lo:hi],
                 in_=x_grouped[a][:, lo:hi, :].rearrange("p n t -> p (n t)"),
             )
 
-        def gather_words(a, lo=0, hi=E, at=None):
-            words = place([P, (hi - lo) * C], U32, f"slot_words_{a}_{lo}", at)
-            start = (A - 1 - a) * T
-            window = x_words[:, start : start + WINDOW]
-            nc.vector.tensor_copy(words[:], window.indirect(offs_tile[:, lo * C // 16 : hi * C // 16]))
-            for e in range(lo, hi):
-                slot_words.update({(a, e): words[:, (e - lo) * C : (e - lo + 1) * C]})
+        def gather_words(a, at=None):
+            words = tile([P, SLOTS], U32, f"slot_words_{a}", at)
+            start = (PASSES - 1 - a) * T
+            nc.vector.tensor_copy(words[:], x_words[:, start : start + WINDOW].indirect(offs_tile[:]))
+            slot_words.update({a: words})
 
-        def gather_scales(at=None):
-            scales = place([P, SLOTS], U8, "slot_scales", at)
-            nc.vector.tensor_copy(scales[:], x_scales[:].indirect(offs_tile[:]))
-            held.update({"slot_scales": scales})
+        def stage(first, count):
+            grouped = tile([P, count, N, PACK], BF16, f"w_grouped_{first}")
+            w_grouped.update({first + j: (grouped, j) for j in range(count)})
 
-        def group(name, count, at=None):
-            return place([P, count, N, PACK], BF16, name, at)
-
-        def seat(tile, pieces, first=0):
-            for j, piece in enumerate(pieces):
-                w_grouped.update({piece: (tile, first + j)})
-
-        def interleave(copy, first, count):
+        def interleave_w(copy, first, count):
             raw, i = w_raw[first]
             grouped, j = w_grouped[first]
             copy(
-                out=grouped[:, j : j + count].rearrange("p u (c i) t -> p u c t i", i=4),
-                in_=raw[:, i : i + count].rearrange("p u t (c i) -> p u c t i", i=4),
+                out=grouped[:, j : j + count].rearrange("p u (c i) t -> p u c t i", i=RUN),
+                in_=raw[:, i : i + count].rearrange("p u t (c i) -> p u c t i", i=RUN),
             )
 
-        def interleave_part(copy, piece, lo=0, hi=N):
+        def interleave_features(copy, piece, lo, hi):
             raw, i = w_raw[piece]
             grouped, j = w_grouped[piece]
             copy(
-                out=grouped[:, j, lo:hi].rearrange("p (c i) t -> p c t i", i=4),
-                in_=raw[:, i, :, lo:hi].rearrange("p t (c i) -> p c t i", i=4),
+                out=grouped[:, j, lo:hi].rearrange("p (c i) t -> p c t i", i=RUN),
+                in_=raw[:, i, :, lo:hi].rearrange("p t (c i) -> p c t i", i=RUN),
             )
 
-        def quantise_w(pieces, at=None):
-            grouped, j = w_grouped[pieces[0]]
-            width = len(pieces) * N
-            words = place([P, width], U32, f"w_words_{pieces[0]}", at)
-            scales = keep.tile([P, width], U8, name=f"w_scales_{pieces[0]}", align_bytes=64)
+        def quantise_w(first, count, at=None):
+            grouped, j = w_grouped[first]
+            words = tile([P, count * N], U32, f"w_words_{first}", at)
+            scales = tile([P, count * N], U8, f"w_scales_{first}")
             nc.vector.quantize_mx(
                 out=words[:].bitcast(FP8X4),
                 scales=scales[:],
-                in_=grouped[:, j : j + len(pieces)].rearrange("p u n t -> p (u n t)"),
+                in_=grouped[:, j : j + count].rearrange("p u n t -> p (u n t)"),
             )
-            for i, piece in enumerate(pieces):
-                w_codes.update({piece: (words[:, i * N : (i + 1) * N], scales[:, i * N : (i + 1) * N])})
+            for i in range(count):
+                w_codes.update({first + i: (words[:, i * N : (i + 1) * N], scales[:, i * N : (i + 1) * N])})
 
-        def multiply(pieces):
-            for piece in pieces:
-                e, a = divmod(piece, A)
+        def multiply(first, last):
+            for piece in range(first, last):
+                e, a = divmod(piece, PASSES)
                 words, scales = w_codes[piece]
-                done = len([other for other in multiplied if other // A == e])
-                multiplied.append(piece)
                 nc.tensor.matmul_mx(
                     out=sums[e][:],
                     lhsT=words.bitcast(FP8X4),
                     lhsT_scale=scales,
-                    rhs=slot_words[(a, e)].bitcast(FP8X4),
-                    rhs_scale=held["slot_scales"][SCALE_ROW * a : P, e * C : (e + 1) * C],
-                    start=(done == 0),
-                    stop=(done == A - 1),
+                    rhs=slot_words[a][:, e * C : (e + 1) * C].bitcast(FP8X4),
+                    rhs_scale=slot_scales[SCALE_ROW * a : P, e * C : (e + 1) * C],
+                    start=(a == 0),
+                    stop=(a == PASSES - 1),
                 )
 
-        def relu(experts):
-            for e in experts:
-                nc.scalar.activation(held["results"][:, e * C : (e + 1) * C], sums[e][:], RELU, bias=bias[:, e : e + 1])
+        def relu(first, last):
+            for e in range(first, last):
+                nc.scalar.activation(results[:, e * C : (e + 1) * C], sums[e][:], RELU, bias=bias[:, e : e + 1])
 
-        def make_results(at=None):
-            held.update({"results": place([P, SLOTS], F32, "results", at)})
-
-        def load_way_back():
-            nc.sync.dma_start(pos1_tile[:], pos1)
-            nc.sync.dma_start(out=gate1[:], in_=gate[0])
-            nc.sync.dma_start(pos2_tile[:], pos2)
-            nc.sync.dma_start(out=gate2[:], in_=gate[1])
-
-        on_scalar = nc.scalar.copy
-        on_vector = nc.vector.tensor_copy
-
-        load_x(0)
+        nc.sync.dma_start(out=x_raw[0][:], in_=x_rows[0])
         nc.sync.dma_start(offs_tile[:], offs)
-        load_x(1)
-        load_x(2)
+        nc.sync.dma_start(out=x_raw[1][:], in_=x_rows[1])
+        nc.sync.dma_start(out=x_raw[2][:], in_=x_rows[2])
         nc.sync.dma_start(out=bias[:], in_=b)
         for first in range(0, 22, 2):
             load_w(first, 2, at={0: 1 * KIB, 14: 8 * KIB}.get(first))
         load_w(22, 1)
         load_w(23, 1)
-        load_way_back()
+        nc.sync.dma_start(pos1_tile[:], pos1)
+        nc.sync.dma_start(pos2_tile[:], pos2)
+        nc.sync.dma_start(out=gate1[:], in_=gate[0])
+        nc.sync.dma_start(out=gate2[:], in_=gate[1])
 
         nc.vector.memset(x_scales[:].bitcast(I32), 0)
-        nc.vector.memset(x_words[:, A * T :].bitcast(I32), 0)
-        group_x(0)
-        interleave_x(on_vector, 0, 0, 256)
-        interleave_x(on_vector, 0, 256, 352)
-        interleave_x(on_scalar, 0, 352, T)
+        nc.vector.memset(x_words[:, PASSES * T :].bitcast(I32), 0)
+        interleave_x(vector_copy, 0, 0, 256)
+        interleave_x(vector_copy, 0, 256, 352)
+        interleave_x(scalar_copy, 0, 352, T)
         quantise_x(0, 0, 256)
         quantise_x(0, 256, T)
         gather_words(0)
-        group_x(1)
-        interleave_x(on_scalar, 1, 256, T)
-        interleave_x(on_scalar, 1, 128, 256)
-        interleave_x(on_vector, 1, 0, 128)
+        interleave_x(scalar_copy, 1, 256, T)
+        interleave_x(scalar_copy, 1, 128, 256)
+        interleave_x(vector_copy, 1, 0, 128)
         quantise_x(1, 256, T)
         quantise_x(1, 0, 256)
-        group_x(2)
-        interleave_x(on_vector, 2, 0, 256)
-        interleave_x(on_scalar, 2, 256, T)
+        interleave_x(vector_copy, 2, 0, 256)
+        interleave_x(scalar_copy, 2, 256, T)
         gather_words(1)
-        quantise_x(2)
-        seat(group("g0", 2), (0, 1))
-        interleave(on_scalar, 0, 2)
-        quantise_w((0, 1))
+        quantise_x(2, 0, T)
+        stage(0, 2)
+        interleave_w(scalar_copy, 0, 2)
+        quantise_w(0, 2)
         gather_words(2, at=0)
-        gather_scales(at=4 * KIB)
+        slot_scales = tile([P, SLOTS], U8, "slot_scales", 4 * KIB)
+        nc.vector.tensor_copy(slot_scales[:], x_scales[:].indirect(offs_tile[:]))
+
         for first in (2, 6, 10):
-            seat(group(f"g{first}", 4), range(first, first + 4))
-            interleave(on_scalar, first, 2)
-            interleave(on_scalar, first + 2, 2)
+            stage(first, 4)
+            interleave_w(scalar_copy, first, 2)
+            interleave_w(scalar_copy, first + 2, 2)
             if first < 10:
-                quantise_w(range(first, first + 4))
-        multiply(range(10))
-        seat(group("g14", 4), range(14, 18))
-        interleave(on_scalar, 14, 2)
-        make_results(at=6 * KIB)
-        relu(range(3))
-        interleave(on_vector, 16, 2)
-        quantise_w((10, 11, 12, 13), at=10 * KIB)
-        quantise_w((14, 15, 16, 17))
-        multiply(range(10, 18))
-        seat(group("g18", 2), (18, 19))
-        interleave(on_scalar, 18, 2)
-        seat(group("g20", 2), (20, 21))
-        interleave(on_vector, 20, 2)
-        quantise_w((18, 19))
-        quantise_w((20, 21))
-        multiply(range(18, 22))
-        relu((3, 4, 5))
-        seat(group("g22", 1), (22,))
-        interleave_part(on_scalar, 22)
-        seat(group("g23", 1), (23,))
-        interleave_part(on_vector, 23, 32, N)
-        interleave_part(on_scalar, 23, 0, 32)
-        quantise_w((22,))
-        multiply((22,))
-        quantise_w((23,))
-        multiply((23,))
-        relu((6, 7))
+                quantise_w(first, 4)
+        multiply(0, 10)
+        stage(14, 4)
+        interleave_w(scalar_copy, 14, 2)
+        results = tile([P, SLOTS], F32, "results", 6 * KIB)
+        relu(0, 3)
+        interleave_w(vector_copy, 16, 2)
+        quantise_w(10, 4, at=10 * KIB)
+        quantise_w(14, 4)
+        multiply(10, 18)
+        stage(18, 2)
+        interleave_w(scalar_copy, 18, 2)
+        stage(20, 2)
+        interleave_w(vector_copy, 20, 2)
+        quantise_w(18, 2)
+        quantise_w(20, 2)
+        multiply(18, 22)
+        relu(3, 6)
+        stage(22, 1)
+        interleave_features(scalar_copy, 22, 0, N)
+        stage(23, 1)
+        interleave_features(vector_copy, 23, 32, N)
+        interleave_features(scalar_copy, 23, 0, 32)
+        quantise_w(22, 1)
+        multiply(22, 23)
+        quantise_w(23, 1)
+        multiply(23, 24)
+        relu(6, 8)
 
-
-        results = held["results"]
         halves = ((0, T // 2), (T // 2, T))
-        y1 = keep.tile([P, T], F32, name="y1")
-        nc.vector.tensor_tensor(y1[:], results[:].indirect(pos1_tile[:]), gate1[:], MULT)
-        y2 = []
+        first_term = tile([P, T], F32, "first_term")
+        nc.vector.tensor_tensor(first_term[:], results[:].indirect(pos1_tile[:]), gate1[:], MULT)
+        second_terms = []
         for lo, hi in halves:
-            part = keep.tile([P, hi - lo], F32, name=f"y2_{lo}")
-            nc.vector.tensor_tensor(part[:], results[:].indirect(pos2_tile[:, lo // 16 : hi // 16]), gate2[:, lo:hi], MULT)
-            y2.append(part)
-        for (lo, hi), part in zip(halves, y2):
-            y = keep.tile([P, hi - lo], F32, name=f"y_{lo}")
-            nc.vector.tensor_tensor(y[:], y1[:, lo:hi], part[:], ADD)
+            fetched = tile([P, hi - lo], F32, f"fetched_{lo}")
+            nc.scalar.activation(fetched[:], results[:].indirect(pos2_tile[:, lo // LANES : hi // LANES]), COPY)
+            term = tile([P, hi - lo], F32, f"second_term_{lo}")
+            nc.vector.tensor_tensor(term[:], fetched[:], gate2[:, lo:hi], MULT)
+            second_terms.append(term)
+        for (lo, hi), term in zip(halves, second_terms):
+            y = tile([P, hi - lo], F32, f"y_{lo}")
+            nc.vector.tensor_tensor(y[:], first_term[:, lo:hi], term[:], ADD)
             nc.sync.dma_start(out=out[:, lo:hi], in_=y[:])

@@ -25,7 +25,7 @@ MULT = mybir.AluOpType.mult
 
 WINDOW = 1408
 SCALE_ROW = 4
-RUN = 4
+RUN = 2
 KIB = 1024
 
 
@@ -145,8 +145,8 @@ def tile_routed_moe_kernel(tc, xT, w, b, gate, offs, pos1, pos2, out):
         load_w(22, 1)
         load_w(23, 1)
         nc.sync.dma_start(pos1_tile[:], pos1)
-        nc.sync.dma_start(pos2_tile[:], pos2)
         nc.sync.dma_start(out=gate1[:], in_=gate[0])
+        nc.sync.dma_start(pos2_tile[:], pos2)
         nc.sync.dma_start(out=gate2[:], in_=gate[1])
 
         nc.vector.memset(x_scales[:].bitcast(I32), 0)

@@ -22,6 +22,7 @@ RELU = mybir.ActivationFunctionType.Relu
 COPY = mybir.ActivationFunctionType.Copy
 ADD = mybir.AluOpType.add
 MULT = mybir.AluOpType.mult
+MAX = mybir.AluOpType.max
 
 WINDOW = 1408
 SCALE_ROW = 4
@@ -60,10 +61,10 @@ def tile_routed_moe_kernel(tc, xT, w, b, gate, offs, pos1, pos2, out):
         w_rows = w.flatten_outer_dims().rearrange("(u p t) n -> p u (t n)", p=P, t=PACK)
         w_raw, w_grouped, w_codes, slot_words = {}, {}, {}, {}
 
-        def load_w(first, count, at=None):
+        def load_w(first, count, step=1, at=None):
             raw = tile([P, count, PACK, N], F32, f"w_raw_{first}", at)
-            nc.sync.dma_start(out=raw[:].rearrange("p u t n -> p u (t n)"), in_=w_rows[:, first : first + count, :])
-            w_raw.update({first + j: (raw, j) for j in range(count)})
+            nc.sync.dma_start(out=raw[:].rearrange("p u t n -> p u (t n)"), in_=w_rows[:, first : first + step * (count - 1) + 1 : step, :])
+            w_raw.update({first + step * j: (raw, j) for j in range(count)})
 
         def interleave_x(copy, a, lo, hi):
             copy(
@@ -85,9 +86,9 @@ def tile_routed_moe_kernel(tc, xT, w, b, gate, offs, pos1, pos2, out):
             nc.vector.tensor_copy(words[:], x_words[:, start : start + WINDOW].indirect(offs_tile[:]))
             slot_words.update({a: words})
 
-        def stage(first, count):
-            grouped = tile([P, count, N, PACK], BF16, f"w_grouped_{first}")
-            w_grouped.update({first + j: (grouped, j) for j in range(count)})
+        def stage(first, count, step=1, at=None):
+            grouped = tile([P, count, N, PACK], BF16, f"w_grouped_{first}", at)
+            w_grouped.update({first + step * j: (grouped, j) for j in range(count)})
 
         def interleave_w(copy, first, count):
             raw, i = w_raw[first]
@@ -105,7 +106,7 @@ def tile_routed_moe_kernel(tc, xT, w, b, gate, offs, pos1, pos2, out):
                 in_=raw[:, i, :, lo:hi].rearrange("p t (c i) -> p c t i", i=RUN),
             )
 
-        def quantise_w(first, count, at=None):
+        def quantise_w(first, count, step=1, at=None):
             grouped, j = w_grouped[first]
             words = tile([P, count * N], U32, f"w_words_{first}", at)
             scales = tile([P, count * N], U8, f"w_scales_{first}")
@@ -115,7 +116,7 @@ def tile_routed_moe_kernel(tc, xT, w, b, gate, offs, pos1, pos2, out):
                 in_=grouped[:, j : j + count].rearrange("p u n t -> p (u n t)"),
             )
             for i in range(count):
-                w_codes.update({first + i: (words[:, i * N : (i + 1) * N], scales[:, i * N : (i + 1) * N])})
+                w_codes.update({first + step * i: (words[:, i * N : (i + 1) * N], scales[:, i * N : (i + 1) * N])})
 
         def multiply(first, last):
             for piece in range(first, last):
@@ -131,18 +132,22 @@ def tile_routed_moe_kernel(tc, xT, w, b, gate, offs, pos1, pos2, out):
                     stop=(a == PASSES - 1),
                 )
 
-        def relu(first, last):
-            for e in range(first, last):
-                nc.scalar.activation(results[:, e * C : (e + 1) * C], sums[e][:], RELU, bias=bias[:, e : e + 1])
+        def scalar_relu(e):
+            nc.scalar.activation(results[:, e * C : (e + 1) * C], sums[e][:], RELU, bias=bias[:, e : e + 1])
+
+        def vector_relu(e):
+            nc.vector.tensor_scalar(results[:, e * C : (e + 1) * C], sums[e][:], bias[:, e : e + 1], 0.0, ADD, MAX)
 
         nc.sync.dma_start(out=x_raw[0][:], in_=x_rows[0])
         nc.sync.dma_start(offs_tile[:], offs)
         nc.sync.dma_start(out=x_raw[1][:], in_=x_rows[1])
         nc.sync.dma_start(out=x_raw[2][:], in_=x_rows[2])
         nc.sync.dma_start(out=bias[:], in_=b)
-        for first in range(0, 22, 2):
-            load_w(first, 2, at={0: 1 * KIB, 14: 8 * KIB}.get(first))
-        load_w(22, 1)
+        load_w(0, 2, at=1 * KIB)
+        for first in (2, 4, 6, 8, 10, 12, 15, 18, 21):
+            load_w(first, 2)
+        load_w(14, 2, step=3)
+        load_w(20, 1)
         load_w(23, 1)
         nc.sync.dma_start(pos1_tile[:], pos1)
         nc.sync.dma_start(out=gate1[:], in_=gate[0])
@@ -174,38 +179,41 @@ def tile_routed_moe_kernel(tc, xT, w, b, gate, offs, pos1, pos2, out):
         nc.vector.tensor_copy(slot_scales[:], x_scales[:].indirect(offs_tile[:]))
 
         for first in (2, 6, 10):
-            stage(first, 4)
+            stage(first, 4, at={10: 8 * KIB}.get(first))
             interleave_w(scalar_copy, first, 2)
             interleave_w(scalar_copy, first + 2, 2)
-            if first < 10:
-                quantise_w(first, 4)
-        multiply(0, 10)
-        stage(14, 4)
-        interleave_w(scalar_copy, 14, 2)
-        results = tile([P, SLOTS], F32, "results", 6 * KIB)
-        relu(0, 3)
-        interleave_w(vector_copy, 16, 2)
-        quantise_w(10, 4, at=10 * KIB)
-        quantise_w(14, 4)
-        multiply(10, 18)
-        stage(18, 2)
-        interleave_w(scalar_copy, 18, 2)
-        stage(20, 2)
-        interleave_w(vector_copy, 20, 2)
-        quantise_w(18, 2)
-        quantise_w(20, 2)
-        multiply(18, 22)
-        relu(3, 6)
-        stage(22, 1)
-        interleave_features(scalar_copy, 22, 0, N)
+            quantise_w(first, 4)
+        multiply(0, 14)
+        results = tile([P, SLOTS], F32, "results", 8 * KIB)
+        for e in range(4):
+            vector_relu(e)
+        for first in (15, 18, 21):
+            stage(first, 2)
+            interleave_w(scalar_copy, first, 2)
+            if first < 21:
+                quantise_w(first, 2)
+                multiply(first, first + 2)
+        stage(14, 2, step=3)
+        interleave_features(scalar_copy, 14, 0, N)
+        interleave_features(vector_copy, 17, 0, N)
+        quantise_w(21, 2)
+        multiply(21, 23)
+        quantise_w(14, 2, step=3)
+        multiply(14, 15)
+        multiply(17, 18)
+        stage(20, 1)
+        interleave_features(scalar_copy, 20, 0, N)
         stage(23, 1)
-        interleave_features(vector_copy, 23, 32, N)
-        interleave_features(scalar_copy, 23, 0, 32)
-        quantise_w(22, 1)
-        multiply(22, 23)
+        interleave_features(vector_copy, 23, 64, N)
+        interleave_features(scalar_copy, 23, 0, 64)
+        quantise_w(20, 1)
+        multiply(20, 21)
         quantise_w(23, 1)
         multiply(23, 24)
-        relu(6, 8)
+        scalar_relu(4)
+        scalar_relu(5)
+        vector_relu(6)
+        scalar_relu(7)
 
         halves = ((0, T // 2), (T // 2, T))
         first_term = tile([P, T], F32, "first_term")

@@ -142,13 +142,12 @@ def tile_routed_moe_kernel(tc, xT, w, b, gate, offs, pos1, pos2, out):
         nc.sync.dma_start(offs_tile[:], offs)
         nc.sync.dma_start(out=x_raw[1][:], in_=x_rows[1])
         nc.sync.dma_start(out=x_raw[2][:], in_=x_rows[2])
-        nc.sync.dma_start(out=bias[:], in_=b)
         load_w(0, 2, at=1 * KIB)
-        for first in (2, 4, 6, 8, 10, 12, 15, 18, 21):
+        for first in range(2, 22, 2):
             load_w(first, 2)
-        load_w(14, 2, step=3)
-        load_w(20, 1)
-        load_w(23, 1)
+        load_w(22, 1)
+        load_w(23, 1, at=8 * KIB)
+        nc.sync.dma_start(out=bias[:], in_=b)
         nc.sync.dma_start(pos1_tile[:], pos1)
         nc.sync.dma_start(out=gate1[:], in_=gate[0])
         nc.sync.dma_start(pos2_tile[:], pos2)
@@ -178,42 +177,33 @@ def tile_routed_moe_kernel(tc, xT, w, b, gate, offs, pos1, pos2, out):
         slot_scales = tile([P, SLOTS], U8, "slot_scales", 4 * KIB)
         nc.vector.tensor_copy(slot_scales[:], x_scales[:].indirect(offs_tile[:]))
 
-        for first in (2, 6, 10):
-            stage(first, 4, at={10: 8 * KIB}.get(first))
+        for first in (2, 6, 10, 14):
+            stage(first, 4)
             interleave_w(scalar_copy, first, 2)
             interleave_w(scalar_copy, first + 2, 2)
             quantise_w(first, 4)
-        multiply(0, 14)
-        results = tile([P, SLOTS], F32, "results", 8 * KIB)
-        for e in range(4):
-            vector_relu(e)
-        for first in (15, 18, 21):
+        multiply(0, 18)
+        for first in (18, 20):
             stage(first, 2)
-            interleave_w(scalar_copy, first, 2)
-            if first < 21:
-                quantise_w(first, 2)
-                multiply(first, first + 2)
-        stage(14, 2, step=3)
-        interleave_features(scalar_copy, 14, 0, N)
-        interleave_features(vector_copy, 17, 0, N)
-        quantise_w(21, 2)
-        multiply(21, 23)
-        quantise_w(14, 2, step=3)
-        multiply(14, 15)
-        multiply(17, 18)
-        stage(20, 1)
-        interleave_features(scalar_copy, 20, 0, N)
+            interleave_features(scalar_copy, first, 0, N)
+            interleave_features(vector_copy, first + 1, 0, N)
+        quantise_w(18, 2)
+        quantise_w(20, 2)
+        multiply(18, 22)
+        stage(22, 1)
+        interleave_features(scalar_copy, 22, 0, N)
         stage(23, 1)
         interleave_features(vector_copy, 23, 64, N)
         interleave_features(scalar_copy, 23, 0, 64)
-        quantise_w(20, 1)
-        multiply(20, 21)
+        quantise_w(22, 1)
+        multiply(22, 23)
         quantise_w(23, 1)
         multiply(23, 24)
-        scalar_relu(4)
-        scalar_relu(5)
-        vector_relu(6)
-        scalar_relu(7)
+        results = tile([P, SLOTS], F32, "results", 8 * KIB)
+        for e in range(4):
+            vector_relu(e)
+        for e in range(4, E):
+            scalar_relu(e)
 
         halves = ((0, T // 2), (T // 2, T))
         first_term = tile([P, T], F32, "first_term")

@@ -174,19 +174,29 @@ def tile_routed_moe_kernel(tc, xT, w, b, gate, offs, pos1, pos2, out):
         interleave_w(scalar_copy, 0, 2)
         quantise_w(0, 2)
         gather_words(2, at=0)
-        slot_scales = tile([P, SLOTS], U8, "slot_scales", 4 * KIB)
-        nc.vector.tensor_copy(slot_scales[:], x_scales[:].indirect(offs_tile[:]))
 
-        for first in (2, 6, 10, 14):
+        for first in (2, 6):
             stage(first, 4)
             interleave_w(scalar_copy, first, 2)
             interleave_w(scalar_copy, first + 2, 2)
             quantise_w(first, 4)
-        multiply(0, 18)
-        for first in (18, 20):
+        stage(10, 2, at=12 * KIB)
+        interleave_w(vector_copy, 10, 2)
+        quantise_w(10, 2)
+        slot_scales = tile([P, SLOTS], U8, "slot_scales", 12 * KIB)
+        nc.vector.tensor_copy(slot_scales[:], x_scales[:].indirect(offs_tile[:]))
+        stage(12, 4)
+        interleave_w(scalar_copy, 12, 2)
+        interleave_w(scalar_copy, 14, 2)
+        quantise_w(12, 4)
+        for first in (16, 18):
             stage(first, 2)
-            interleave_features(scalar_copy, first, 0, N)
-            interleave_features(vector_copy, first + 1, 0, N)
+            interleave_w(scalar_copy, first, 2)
+        quantise_w(16, 2)
+        multiply(0, 18)
+        stage(20, 2)
+        interleave_features(scalar_copy, 20, 0, N)
+        interleave_features(vector_copy, 21, 0, N)
         quantise_w(18, 2)
         quantise_w(20, 2)
         multiply(18, 22)

@@ -210,9 +210,9 @@ def tile_routed_moe_kernel(tc, xT, w, b, gate, offs, pos1, pos2, out):
         quantise_w(23, 1)
         multiply(23, 24)
         results = tile([P, SLOTS], F32, "results", 8 * KIB)
-        for e in range(4):
+        for e in range(3):
             vector_relu(e)
-        for e in range(4, E):
+        for e in range(3, E):
             scalar_relu(e)
 
         halves = ((0, T // 2), (T // 2, T))

@@ -146,7 +146,7 @@ def tile_routed_moe_kernel(tc, xT, w, b, gate, offs, pos1, pos2, out):
         for first in range(2, 22, 2):
             load_w(first, 2)
         load_w(22, 1)
-        load_w(23, 1, at=8 * KIB)
+        load_w(23, 1)
         nc.sync.dma_start(out=bias[:], in_=b)
         nc.sync.dma_start(pos1_tile[:], pos1)
         nc.sync.dma_start(out=gate1[:], in_=gate[0])
@@ -203,13 +203,13 @@ def tile_routed_moe_kernel(tc, xT, w, b, gate, offs, pos1, pos2, out):
         stage(22, 1)
         interleave_features(scalar_copy, 22, 0, N)
         stage(23, 1)
-        interleave_features(vector_copy, 23, 64, N)
-        interleave_features(scalar_copy, 23, 0, 64)
+        interleave_features(vector_copy, 23, 48, N)
+        interleave_features(scalar_copy, 23, 0, 48)
         quantise_w(22, 1)
         multiply(22, 23)
         quantise_w(23, 1)
         multiply(23, 24)
-        results = tile([P, SLOTS], F32, "results", 8 * KIB)
+        results = tile([P, SLOTS], F32, "results")
         for e in range(3):
             vector_relu(e)
         for e in range(3, E):

@@ -176,23 +176,22 @@ def tile_routed_moe_kernel(tc, xT, w, b, gate, offs, pos1, pos2, out):
         gather_words(2, at=0)
 
         for first in (2, 6):
-            stage(first, 4)
+            stage(first, 4, at={6: 12 * KIB}.get(first))
             interleave_w(scalar_copy, first, 2)
             interleave_w(scalar_copy, first + 2, 2)
             quantise_w(first, 4)
-        stage(10, 2, at=12 * KIB)
-        interleave_w(vector_copy, 10, 2)
-        quantise_w(10, 2)
+        stage(10, 4)
+        interleave_features(scalar_copy, 10, 0, N)
+        interleave_features(vector_copy, 11, 0, N)
         slot_scales = tile([P, SLOTS], U8, "slot_scales", 12 * KIB)
         nc.vector.tensor_copy(slot_scales[:], x_scales[:].indirect(offs_tile[:]))
-        stage(12, 4)
         interleave_w(scalar_copy, 12, 2)
-        interleave_w(scalar_copy, 14, 2)
-        quantise_w(12, 4)
-        for first in (16, 18):
+        quantise_w(10, 4)
+        for first in (14, 16, 18):
             stage(first, 2)
             interleave_w(scalar_copy, first, 2)
-        quantise_w(16, 2)
+            if first < 18:
+                quantise_w(first, 2)
         multiply(0, 18)
         stage(20, 2)
         interleave_features(scalar_copy, 20, 0, N)
@@ -203,8 +202,8 @@ def tile_routed_moe_kernel(tc, xT, w, b, gate, offs, pos1, pos2, out):
         stage(22, 1)
         interleave_features(scalar_copy, 22, 0, N)
         stage(23, 1)
-        interleave_features(vector_copy, 23, 48, N)
-        interleave_features(scalar_copy, 23, 0, 48)
+        interleave_features(vector_copy, 23, 64, N)
+        interleave_features(scalar_copy, 23, 0, 64)
         quantise_w(22, 1)
         multiply(22, 23)
         quantise_w(23, 1)

@@ -53,7 +53,7 @@ def tile_routed_moe_kernel(tc, xT, w, b, gate, offs, pos1, pos2, out):
         gate2 = tile([P, T], F32, "gate2")
         x_scales = tile([P, WINDOW], U8, "x_scales")
         x_words = tile([P, (PASSES - 1) * T + WINDOW], U32, "x_words")
-        x_raw = [tile([P, PACK, T], F32, f"x_raw_{a}") for a in range(PASSES)]
+        x_raw = [tile([P, PACK, T], F32, f"x_raw_{a}", {2: 0}.get(a)) for a in range(PASSES)]
         x_grouped = [tile([P, T, PACK], BF16, f"x_grouped_{a}") for a in range(PASSES)]
         sums = [psum.tile([N, C], F32, name=f"sums_{e}") for e in range(E)]
 
@@ -142,9 +142,8 @@ def tile_routed_moe_kernel(tc, xT, w, b, gate, offs, pos1, pos2, out):
         nc.sync.dma_start(offs_tile[:], offs)
         nc.sync.dma_start(out=x_raw[1][:], in_=x_rows[1])
         nc.sync.dma_start(out=x_raw[2][:], in_=x_rows[2])
-        load_w(0, 2, at=1 * KIB)
-        for first in range(2, 22, 2):
-            load_w(first, 2)
+        for first in range(0, 22, 2):
+            load_w(first, 2, at={2: 8 * KIB, 8: 12 * KIB}.get(first))
         load_w(22, 1)
         load_w(23, 1)
         nc.sync.dma_start(out=bias[:], in_=b)
@@ -166,27 +165,31 @@ def tile_routed_moe_kernel(tc, xT, w, b, gate, offs, pos1, pos2, out):
         interleave_x(vector_copy, 1, 0, 128)
         quantise_x(1, 256, T)
         quantise_x(1, 0, 256)
-        interleave_x(vector_copy, 2, 0, 256)
-        interleave_x(scalar_copy, 2, 256, T)
-        gather_words(1)
-        quantise_x(2, 0, T)
-        stage(0, 2)
-        interleave_w(scalar_copy, 0, 2)
-        quantise_w(0, 2)
-        gather_words(2, at=0)
+        interleave_x(vector_copy, 2, 0, 128)
+        interleave_x(vector_copy, 2, 256, 384)
+        interleave_x(scalar_copy, 2, 128, 256)
+        interleave_x(scalar_copy, 2, 384, T)
+        quantise_x(2, 0, 256)
+        gather_words(1, at=0)
+        quantise_x(2, 256, T)
 
-        for first in (2, 6):
-            stage(first, 4, at={6: 12 * KIB}.get(first))
+        for first in (0, 4):
+            stage(first, 4)
             interleave_w(scalar_copy, first, 2)
             interleave_w(scalar_copy, first + 2, 2)
             quantise_w(first, 4)
-        stage(10, 4)
-        interleave_features(scalar_copy, 10, 0, N)
-        interleave_features(vector_copy, 11, 0, N)
+            if first == 0:
+                gather_words(2, at=8 * KIB)
+        stage(8, 3)
+        stage(11, 3)
+        interleave_w(scalar_copy, 8, 2)
         slot_scales = tile([P, SLOTS], U8, "slot_scales", 12 * KIB)
         nc.vector.tensor_copy(slot_scales[:], x_scales[:].indirect(offs_tile[:]))
+        interleave_features(vector_copy, 11, 0, N)
+        interleave_features(scalar_copy, 10, 0, N)
+        quantise_w(8, 3)
         interleave_w(scalar_copy, 12, 2)
-        quantise_w(10, 4)
+        quantise_w(11, 3)
         for first in (14, 16, 18):
             stage(first, 2)
             interleave_w(scalar_copy, first, 2)

@@ -53,7 +53,7 @@ def tile_routed_moe_kernel(tc, xT, w, b, gate, offs, pos1, pos2, out):
         gate2 = tile([P, T], F32, "gate2")
         x_scales = tile([P, WINDOW], U8, "x_scales")
         x_words = tile([P, (PASSES - 1) * T + WINDOW], U32, "x_words")
-        x_raw = [tile([P, PACK, T], F32, f"x_raw_{a}", {2: 0}.get(a)) for a in range(PASSES)]
+        x_raw = [tile([P, PACK, T], F32, f"x_raw_{a}") for a in range(PASSES)]
         x_grouped = [tile([P, T, PACK], BF16, f"x_grouped_{a}") for a in range(PASSES)]
         sums = [psum.tile([N, C], F32, name=f"sums_{e}") for e in range(E)]
 
@@ -165,31 +165,29 @@ def tile_routed_moe_kernel(tc, xT, w, b, gate, offs, pos1, pos2, out):
         interleave_x(vector_copy, 1, 0, 128)
         quantise_x(1, 256, T)
         quantise_x(1, 0, 256)
-        interleave_x(vector_copy, 2, 0, 128)
-        interleave_x(vector_copy, 2, 256, 384)
-        interleave_x(scalar_copy, 2, 128, 256)
-        interleave_x(scalar_copy, 2, 384, T)
-        quantise_x(2, 0, 256)
-        gather_words(1, at=0)
-        quantise_x(2, 256, T)
+        gather_words(1)
+        interleave_x(scalar_copy, 2, 0, T)
 
-        for first in (0, 4):
-            stage(first, 4)
-            interleave_w(scalar_copy, first, 2)
-            interleave_w(scalar_copy, first + 2, 2)
-            quantise_w(first, 4)
-            if first == 0:
-                gather_words(2, at=8 * KIB)
-        stage(8, 3)
-        stage(11, 3)
+        stage(0, 4)
+        interleave_w(vector_copy, 0, 2)
+        quantise_x(2, 0, T)
+        interleave_w(scalar_copy, 2, 2)
+        quantise_w(0, 4)
+        gather_words(2, at=8 * KIB)
+        stage(4, 4)
+        interleave_w(scalar_copy, 4, 2)
+        interleave_w(scalar_copy, 6, 2)
+        quantise_w(4, 4)
+        stage(8, 2)
+        stage(10, 4)
         interleave_w(scalar_copy, 8, 2)
-        slot_scales = tile([P, SLOTS], U8, "slot_scales", 12 * KIB)
-        nc.vector.tensor_copy(slot_scales[:], x_scales[:].indirect(offs_tile[:]))
         interleave_features(vector_copy, 11, 0, N)
         interleave_features(scalar_copy, 10, 0, N)
-        quantise_w(8, 3)
+        quantise_w(8, 2)
+        slot_scales = tile([P, SLOTS], U8, "slot_scales", 12 * KIB)
+        nc.vector.tensor_copy(slot_scales[:], x_scales[:].indirect(offs_tile[:]))
         interleave_w(scalar_copy, 12, 2)
-        quantise_w(11, 3)
+        quantise_w(10, 4)
         for first in (14, 16, 18):
             stage(first, 2)
             interleave_w(scalar_copy, first, 2)

@@ -188,16 +188,18 @@ def tile_routed_moe_kernel(tc, xT, w, b, gate, offs, pos1, pos2, out):
         nc.vector.tensor_copy(slot_scales[:], x_scales[:].indirect(offs_tile[:]))
         interleave_w(scalar_copy, 12, 2)
         quantise_w(10, 4)
-        for first in (14, 16, 18):
+        for first in (14, 16, 18, 20):
             stage(first, 2)
-            interleave_w(scalar_copy, first, 2)
-            if first < 18:
-                quantise_w(first, 2)
+        interleave_w(scalar_copy, 14, 2)
+        quantise_w(14, 2)
+        interleave_w(scalar_copy, 16, 2)
+        interleave_features(vector_copy, 19, 0, N)
+        quantise_w(16, 2)
         multiply(0, 18)
-        stage(20, 2)
+        interleave_features(scalar_copy, 18, 0, N)
+        quantise_w(18, 2)
         interleave_features(scalar_copy, 20, 0, N)
         interleave_features(vector_copy, 21, 0, N)
-        quantise_w(18, 2)
         quantise_w(20, 2)
         multiply(18, 22)
         stage(22, 1)

@@ -205,8 +205,8 @@ def tile_routed_moe_kernel(tc, xT, w, b, gate, offs, pos1, pos2, out):
         stage(22, 1)
         interleave_features(scalar_copy, 22, 0, N)
         stage(23, 1)
-        interleave_features(vector_copy, 23, 64, N)
-        interleave_features(scalar_copy, 23, 0, 64)
+        interleave_features(vector_copy, 23, 48, N)
+        interleave_features(scalar_copy, 23, 0, 48)
         quantise_w(22, 1)
         multiply(22, 23)
         quantise_w(23, 1)

@@ -28,6 +28,7 @@ WINDOW = 1408
 SCALE_ROW = 4
 RUN = 2
 KIB = 1024
+ALIGN = 256
 
 
 def tile_routed_moe_kernel(tc, xT, w, b, gate, offs, pos1, pos2, out):
@@ -42,8 +43,8 @@ def tile_routed_moe_kernel(tc, xT, w, b, gate, offs, pos1, pos2, out):
 
         def tile(shape, dtype, name, at=None):
             if at is None:
-                return keep.tile(shape, dtype, name=name, align_bytes=64)
-            return shared.tile(shape, dtype, name=name, align_bytes=64, offset=at)
+                return keep.tile(shape, dtype, name=name, align_bytes=ALIGN)
+            return shared.tile(shape, dtype, name=name, align_bytes=ALIGN, offset=at)
 
         offs_tile = keep.tile([P, SLOTS // LANES], U16, name="offs_tile")
         pos1_tile = keep.tile([P, T // LANES], U16, name="pos1_tile")

@@ -180,36 +180,34 @@ def tile_routed_moe_kernel(tc, xT, w, b, gate, offs, pos1, pos2, out):
         interleave_w(scalar_copy, 6, 2)
         quantise_w(4, 4)
         stage(8, 2)
-        stage(10, 4)
         interleave_w(scalar_copy, 8, 2)
-        interleave_features(vector_copy, 11, 0, N)
-        interleave_features(scalar_copy, 10, 0, N)
         quantise_w(8, 2)
         slot_scales = tile([P, SLOTS], U8, "slot_scales", 12 * KIB)
         nc.vector.tensor_copy(slot_scales[:], x_scales[:].indirect(offs_tile[:]))
+        stage(10, 4)
+        interleave_w(scalar_copy, 10, 2)
         interleave_w(scalar_copy, 12, 2)
         quantise_w(10, 4)
-        for first in (14, 16, 18, 20):
-            stage(first, 2)
+        stage(14, 2)
         interleave_w(scalar_copy, 14, 2)
         quantise_w(14, 2)
-        interleave_w(scalar_copy, 16, 2)
-        interleave_features(vector_copy, 19, 0, N)
-        quantise_w(16, 2)
-        multiply(0, 18)
-        interleave_features(scalar_copy, 18, 0, N)
-        quantise_w(18, 2)
-        interleave_features(scalar_copy, 20, 0, N)
-        interleave_features(vector_copy, 21, 0, N)
-        quantise_w(20, 2)
-        multiply(18, 22)
-        stage(22, 1)
+        stage(16, 1)
+        for first in (17, 19, 21):
+            stage(first, 2)
+        interleave_features(vector_copy, 17, 0, N)
+        interleave_features(scalar_copy, 16, 0, N)
+        quantise_w(16, 1)
+        for first in (18, 20):
+            interleave_features(vector_copy, first + 1, 0, N)
+            interleave_features(scalar_copy, first, 0, N)
+            quantise_w(first - 1, 2)
+        multiply(0, 21)
         interleave_features(scalar_copy, 22, 0, N)
         stage(23, 1)
         interleave_features(vector_copy, 23, 48, N)
         interleave_features(scalar_copy, 23, 0, 48)
-        quantise_w(22, 1)
-        multiply(22, 23)
+        quantise_w(21, 2)
+        multiply(21, 23)
         quantise_w(23, 1)
         multiply(23, 24)
         results = tile([P, SLOTS], F32, "results")

@@ -41,10 +41,10 @@ def tile_routed_moe_kernel(tc, xT, w, b, gate, offs, pos1, pos2, out):
         shared = ctx.enter_context(tc.tile_pool(name="shared", bufs=1))
         psum = ctx.enter_context(tc.psum_pool(name="psum", bufs=1))
 
-        def tile(shape, dtype, name, at=None):
+        def tile(shape, dtype, name, at=None, align=ALIGN):
             if at is None:
-                return keep.tile(shape, dtype, name=name, align_bytes=ALIGN)
-            return shared.tile(shape, dtype, name=name, align_bytes=ALIGN, offset=at)
+                return keep.tile(shape, dtype, name=name, align_bytes=align)
+            return shared.tile(shape, dtype, name=name, align_bytes=align, offset=at)
 
         offs_tile = keep.tile([P, SLOTS // LANES], U16, name="offs_tile")
         pos1_tile = keep.tile([P, T // LANES], U16, name="pos1_tile")
@@ -54,7 +54,7 @@ def tile_routed_moe_kernel(tc, xT, w, b, gate, offs, pos1, pos2, out):
         gate2 = tile([P, T], F32, "gate2")
         x_scales = tile([P, WINDOW], U8, "x_scales")
         x_words = tile([P, (PASSES - 1) * T + WINDOW], U32, "x_words")
-        x_raw = [tile([P, PACK, T], F32, f"x_raw_{a}") for a in range(PASSES)]
+        x_raw = [tile([P, PACK, T], F32, f"x_raw_{a}", align=4 * KIB) for a in range(PASSES)]
         x_grouped = [tile([P, T, PACK], BF16, f"x_grouped_{a}") for a in range(PASSES)]
         sums = [psum.tile([N, C], F32, name=f"sums_{e}") for e in range(E)]
 
@@ -63,7 +63,7 @@ def tile_routed_moe_kernel(tc, xT, w, b, gate, offs, pos1, pos2, out):
         w_raw, w_grouped, w_codes, slot_words = {}, {}, {}, {}
 
         def load_w(first, count, step=1, at=None):
-            raw = tile([P, count, PACK, N], F32, f"w_raw_{first}", at)
+            raw = tile([P, count, PACK, N], F32, f"w_raw_{first}", at, align=min(count * 2, 4) * KIB)
             nc.sync.dma_start(out=raw[:].rearrange("p u t n -> p u (t n)"), in_=w_rows[:, first : first + step * (count - 1) + 1 : step, :])
             w_raw.update({first + step * j: (raw, j) for j in range(count)})
 

@@ -216,17 +216,14 @@ def tile_routed_moe_kernel(tc, xT, w, b, gate, offs, pos1, pos2, out):
         for e in range(3, E):
             scalar_relu(e)
 
-        halves = ((0, T // 2), (T // 2, T))
         first_term = tile([P, T], F32, "first_term")
         nc.vector.tensor_tensor(first_term[:], results[:].indirect(pos1_tile[:]), gate1[:], MULT)
-        second_terms = []
-        for lo, hi in halves:
+        second_term = tile([P, T], F32, "second_term")
+        for lo, hi in ((0, 320), (320, T)):
             fetched = tile([P, hi - lo], F32, f"fetched_{lo}")
             nc.scalar.activation(fetched[:], results[:].indirect(pos2_tile[:, lo // LANES : hi // LANES]), COPY)
-            term = tile([P, hi - lo], F32, f"second_term_{lo}")
-            nc.vector.tensor_tensor(term[:], fetched[:], gate2[:, lo:hi], MULT)
-            second_terms.append(term)
-        for (lo, hi), term in zip(halves, second_terms):
+            nc.vector.tensor_tensor(second_term[:, lo:hi], fetched[:], gate2[:, lo:hi], MULT)
+        for lo, hi in ((0, T // 2), (T // 2, T)):
             y = tile([P, hi - lo], F32, f"y_{lo}")
-            nc.vector.tensor_tensor(y[:], first_term[:, lo:hi], term[:], ADD)
+            nc.vector.tensor_tensor(y[:], first_term[:, lo:hi], second_term[:, lo:hi], ADD)
             nc.sync.dma_start(out=out[:, lo:hi], in_=y[:])

@@ -204,8 +204,8 @@ def tile_routed_moe_kernel(tc, xT, w, b, gate, offs, pos1, pos2, out):
         multiply(0, 21)
         interleave_features(scalar_copy, 22, 0, N)
         stage(23, 1)
-        interleave_features(vector_copy, 23, 48, N)
-        interleave_features(scalar_copy, 23, 0, 48)
+        interleave_features(vector_copy, 23, 64, N)
+        interleave_features(scalar_copy, 23, 0, 64)
         quantise_w(21, 2)
         multiply(21, 23)
         quantise_w(23, 1)

from contextlib import ExitStack

import concourse.mybir as mybir

K, T, E, C, N = 1536, 512, 8, 128, 128
P = 128
PACK = 4
PASSES = K // (P * PACK)
SLOTS = E * C
LANES = 16

FLOPS = 2 * K * N * SLOTS

F32 = mybir.dt.float32
BF16 = mybir.dt.bfloat16
I32 = mybir.dt.int32
U32 = mybir.dt.uint32
U16 = mybir.dt.uint16
U8 = mybir.dt.uint8
FP8X4 = mybir.dt.float8_e4m3fn_x4
RELU = mybir.ActivationFunctionType.Relu
COPY = mybir.ActivationFunctionType.Copy
ADD = mybir.AluOpType.add
MULT = mybir.AluOpType.mult
MAX = mybir.AluOpType.max

WINDOW = 1408
SCALE_ROW = 4
RUN = 2
KIB = 1024
ALIGN = 256


def tile_routed_moe_kernel(tc, xT, w, b, gate, offs, pos1, pos2, out):
    nc = tc.nc
    scalar_copy = nc.scalar.copy
    vector_copy = nc.vector.tensor_copy

    with ExitStack() as ctx:
        keep = ctx.enter_context(tc.tile_pool(name="keep", bufs=1))
        shared = ctx.enter_context(tc.tile_pool(name="shared", bufs=1))
        psum = ctx.enter_context(tc.psum_pool(name="psum", bufs=1))

        def tile(shape, dtype, name, at=None, align=ALIGN):
            if at is None:
                return keep.tile(shape, dtype, name=name, align_bytes=align)
            return shared.tile(shape, dtype, name=name, align_bytes=align, offset=at)

        offs_tile = keep.tile([P, SLOTS // LANES], U16, name="offs_tile")
        pos1_tile = keep.tile([P, T // LANES], U16, name="pos1_tile")
        pos2_tile = keep.tile([P, T // LANES], U16, name="pos2_tile")
        bias = tile([P, E], F32, "bias")
        gate1 = tile([P, T], F32, "gate1")
        gate2 = tile([P, T], F32, "gate2")
        x_scales = tile([P, WINDOW], U8, "x_scales")
        x_words = tile([P, (PASSES - 1) * T + WINDOW], U32, "x_words")
        x_raw = [tile([P, PACK, T], F32, f"x_raw_{a}", align=4 * KIB) for a in range(PASSES)]
        x_grouped = [tile([P, T, PACK], BF16, f"x_grouped_{a}") for a in range(PASSES)]
        sums = [psum.tile([N, C], F32, name=f"sums_{e}") for e in range(E)]

        x_rows = xT.rearrange("(a p t) n -> a p t n", p=P, t=PACK)
        w_rows = w.flatten_outer_dims().rearrange("(u p t) n -> p u (t n)", p=P, t=PACK)
        w_raw, w_grouped, w_codes, slot_words = {}, {}, {}, {}

        def load_w(first, count, step=1, at=None):
            raw = tile([P, count, PACK, N], F32, f"w_raw_{first}", at, align=min(count * 2, 4) * KIB)
            nc.sync.dma_start(out=raw[:].rearrange("p u t n -> p u (t n)"), in_=w_rows[:, first : first + step * (count - 1) + 1 : step, :])
            w_raw.update({first + step * j: (raw, j) for j in range(count)})

        def interleave_x(copy, a, lo, hi):
            copy(
                out=x_grouped[a][:, lo:hi, :].rearrange("p (c i) t -> p c t i", i=RUN),
                in_=x_raw[a][:, :, lo:hi].rearrange("p t (c i) -> p c t i", i=RUN),
            )

        def quantise_x(a, lo, hi):
            start = (PASSES - 1 - a) * T
            nc.vector.quantize_mx(
                out=x_words[:, start + lo : start + hi].bitcast(FP8X4),
                scales=x_scales[SCALE_ROW * a : P, lo:hi],
                in_=x_grouped[a][:, lo:hi, :].rearrange("p n t -> p (n t)"),
            )

        def gather_words(a, at=None):
            words = tile([P, SLOTS], U32, f"slot_words_{a}", at)
            start = (PASSES - 1 - a) * T
            nc.vector.tensor_copy(words[:], x_words[:, start : start + WINDOW].indirect(offs_tile[:]))
            slot_words.update({a: words})

        def stage(first, count, step=1, at=None):
            grouped = tile([P, count, N, PACK], BF16, f"w_grouped_{first}", at)
            w_grouped.update({first + step * j: (grouped, j) for j in range(count)})

        def interleave_w(copy, first, count):
            raw, i = w_raw[first]
            grouped, j = w_grouped[first]
            copy(
                out=grouped[:, j : j + count].rearrange("p u (c i) t -> p u c t i", i=RUN),
                in_=raw[:, i : i + count].rearrange("p u t (c i) -> p u c t i", i=RUN),
            )

        def interleave_features(copy, piece, lo, hi):
            raw, i = w_raw[piece]
            grouped, j = w_grouped[piece]
            copy(
                out=grouped[:, j, lo:hi].rearrange("p (c i) t -> p c t i", i=RUN),
                in_=raw[:, i, :, lo:hi].rearrange("p t (c i) -> p c t i", i=RUN),
            )

        def quantise_w(first, count, step=1, at=None):
            grouped, j = w_grouped[first]
            words = tile([P, count * N], U32, f"w_words_{first}", at)
            scales = tile([P, count * N], U8, f"w_scales_{first}")
            nc.vector.quantize_mx(
                out=words[:].bitcast(FP8X4),
                scales=scales[:],
                in_=grouped[:, j : j + count].rearrange("p u n t -> p (u n t)"),
            )
            for i in range(count):
                w_codes.update({first + step * i: (words[:, i * N : (i + 1) * N], scales[:, i * N : (i + 1) * N])})

        def multiply(first, last):
            for piece in range(first, last):
                e, a = divmod(piece, PASSES)
                words, scales = w_codes[piece]
                nc.tensor.matmul_mx(
                    out=sums[e][:],
                    lhsT=words.bitcast(FP8X4),
                    lhsT_scale=scales,
                    rhs=slot_words[a][:, e * C : (e + 1) * C].bitcast(FP8X4),
                    rhs_scale=slot_scales[SCALE_ROW * a : P, e * C : (e + 1) * C],
                    start=(a == 0),
                    stop=(a == PASSES - 1),
                )

        def scalar_relu(e):
            nc.scalar.activation(results[:, e * C : (e + 1) * C], sums[e][:], RELU, bias=bias[:, e : e + 1])

        def vector_relu(e):
            nc.vector.tensor_scalar(results[:, e * C : (e + 1) * C], sums[e][:], bias[:, e : e + 1], 0.0, ADD, MAX)

        nc.sync.dma_start(out=x_raw[0][:], in_=x_rows[0])
        nc.sync.dma_start(offs_tile[:], offs)
        nc.sync.dma_start(out=x_raw[1][:], in_=x_rows[1])
        nc.sync.dma_start(out=x_raw[2][:], in_=x_rows[2])
        for first in range(0, 22, 2):
            load_w(first, 2, at={2: 8 * KIB, 8: 12 * KIB}.get(first))
        load_w(22, 1)
        load_w(23, 1)
        nc.sync.dma_start(out=bias[:], in_=b)
        nc.sync.dma_start(pos1_tile[:], pos1)
        nc.sync.dma_start(out=gate1[:], in_=gate[0])
        nc.sync.dma_start(pos2_tile[:], pos2)
        nc.sync.dma_start(out=gate2[:], in_=gate[1])

        nc.vector.memset(x_scales[:].bitcast(I32), 0)
        nc.vector.memset(x_words[:, PASSES * T :].bitcast(I32), 0)
        interleave_x(vector_copy, 0, 0, 256)
        interleave_x(vector_copy, 0, 256, 352)
        interleave_x(scalar_copy, 0, 352, T)
        quantise_x(0, 0, 256)
        quantise_x(0, 256, T)
        gather_words(0)
        interleave_x(scalar_copy, 1, 256, T)
        interleave_x(scalar_copy, 1, 128, 256)
        interleave_x(vector_copy, 1, 0, 128)
        quantise_x(1, 256, T)
        quantise_x(1, 0, 256)
        gather_words(1)
        interleave_x(scalar_copy, 2, 0, T)

        stage(0, 4)
        interleave_w(vector_copy, 0, 2)
        quantise_x(2, 0, T)
        interleave_w(scalar_copy, 2, 2)
        quantise_w(0, 4)
        gather_words(2, at=8 * KIB)
        stage(4, 4)
        interleave_w(scalar_copy, 4, 2)
        interleave_w(scalar_copy, 6, 2)
        quantise_w(4, 4)
        stage(8, 2)
        interleave_w(scalar_copy, 8, 2)
        quantise_w(8, 2)
        slot_scales = tile([P, SLOTS], U8, "slot_scales", 12 * KIB)
        nc.vector.tensor_copy(slot_scales[:], x_scales[:].indirect(offs_tile[:]))
        stage(10, 4)
        interleave_w(scalar_copy, 10, 2)
        interleave_w(scalar_copy, 12, 2)
        quantise_w(10, 4)
        stage(14, 2)
        interleave_w(scalar_copy, 14, 2)
        quantise_w(14, 2)
        stage(16, 1)
        for first in (17, 19, 21):
            stage(first, 2)
        interleave_features(vector_copy, 17, 0, N)
        interleave_features(scalar_copy, 16, 0, N)
        quantise_w(16, 1)
        for first in (18, 20):
            interleave_features(vector_copy, first + 1, 0, N)
            interleave_features(scalar_copy, first, 0, N)
            quantise_w(first - 1, 2)
        multiply(0, 21)
        interleave_features(scalar_copy, 22, 0, N)
        stage(23, 1)
        interleave_features(vector_copy, 23, 64, N)
        interleave_features(scalar_copy, 23, 0, 64)
        quantise_w(21, 2)
        multiply(21, 23)
        quantise_w(23, 1)
        multiply(23, 24)
        results = tile([P, SLOTS], F32, "results")
        for e in range(3):
            vector_relu(e)
        for e in range(3, E):
            scalar_relu(e)

        first_term = tile([P, T], F32, "first_term")
        nc.vector.tensor_tensor(first_term[:], results[:].indirect(pos1_tile[:]), gate1[:], MULT)
        second_term = tile([P, T], F32, "second_term")
        for lo, hi in ((0, 320), (320, T)):
            fetched = tile([P, hi - lo], F32, f"fetched_{lo}")
            nc.scalar.activation(fetched[:], results[:].indirect(pos2_tile[:, lo // LANES : hi // LANES]), COPY)
            nc.vector.tensor_tensor(second_term[:, lo:hi], fetched[:], gate2[:, lo:hi], MULT)
        for lo, hi in ((0, T // 2), (T // 2, T)):
            y = tile([P, hi - lo], F32, f"y_{lo}")
            nc.vector.tensor_tensor(y[:], first_term[:, lo:hi], second_term[:, lo:hi], ADD)
            nc.sync.dma_start(out=out[:, lo:hi], in_=y[:])
